import numpy as np
import ml_dtypes


def mxq(x, axis, fmt="e4m3"):
    dtype, down = {"e4m3": (ml_dtypes.float8_e4m3fn, 7), "e5m2": (ml_dtypes.float8_e5m2, 14)}[fmt]
    v = np.moveaxis(np.asarray(x, np.float32).astype(ml_dtypes.bfloat16).astype(np.float64), axis, -1)
    blocks = v.reshape(v.shape[:-1] + (-1, 32))
    amax = np.abs(blocks).max(-1, keepdims=True)
    byte = np.maximum(np.where(amax > 0, np.frexp(amax)[1] - 1 + 127, 0) - down, 1)
    scale = np.exp2(byte - 127.0)
    codes = (blocks / scale).astype(np.float32).astype(dtype).astype(np.float64)
    return np.moveaxis((codes * scale).reshape(v.shape), -1, axis)


WIDE = False


def mx_kscale(k):
    if not WIDE:
        return np.ones(k)
    levels = np.array([10, -10, 5, -5, 0])
    if k % 512:
        return np.exp2(np.random.permutation(np.resize(levels, k // 32))).repeat(32)
    a = np.empty((k // 512, 16))
    for p in range(k // 512):
        a[p, :8] = np.random.permutation(np.resize(levels, 8))
        for g in range(8):
            far = levels[np.abs(levels - a[p, g]) >= 10]
            a[p, g + 8] = far[np.random.randint(len(far))]
    return np.exp2(a.ravel()).repeat(32)


BF16 = ml_dtypes.bfloat16


def bf(x):
    return np.asarray(x, np.float32).astype(BF16)


def f64(x):
    return np.asarray(x).astype(np.float64)


E2M1 = np.array([0.0, 0.5, 1.0, 1.5, 2.0, 3.0, 4.0, 6.0, -0.0, -0.5, -1.0, -1.5, -2.0, -3.0, -4.0, -6.0])


def pack_weight(w, fmt):
    k, n = w.shape
    w = f64(bf(w)).reshape(k // 32, 32, n)
    amax = np.abs(w).max(1)
    if fmt == "e4m3":
        byte = np.frexp(amax)[1] - 1 + 127 - 7
    else:
        mant, ex = np.frexp(amax / 6.0)
        byte = np.where(mant > 0.5, ex, ex - 1) + 127
    byte = np.clip(np.where(amax > 0, byte, 1), 1, 254)
    scaled = (w * np.exp2(127.0 - byte)[:, None, :]).reshape(k, n).astype(np.float32)
    by_word = np.ascontiguousarray(scaled.reshape(k // 512, 128, 4, n).transpose(0, 1, 3, 2))
    if fmt == "e4m3":
        words = by_word.astype(ml_dtypes.float8_e4m3fn).view(np.uint8)
    else:
        c = by_word.astype(ml_dtypes.float4_e2m1fn).view(np.uint8) & 0xF
        words = c[..., 0::2] | (c[..., 1::2] << 4)
    return np.ascontiguousarray(words), np.ascontiguousarray(byte.astype(np.uint8).reshape(k // 512, 16, n))


def unpack_weight(words, scales, fmt):
    g, p, n, _ = words.shape
    if fmt == "e4m3":
        vals = np.ascontiguousarray(words).view(ml_dtypes.float8_e4m3fn).astype(np.float64)
    else:
        nib = np.empty((g, p, n, 4), np.uint8)
        nib[..., 0::2] = words & 0xF
        nib[..., 1::2] = words >> 4
        vals = E2M1[nib]
    vals = vals * np.repeat(np.exp2(scales.astype(np.float64) - 127.0), 8, axis=1)[..., None]
    return vals.transpose(0, 1, 3, 2).reshape(g * 512, n)

E4M3FN = np.array([(-1.0 if i & 128 else 1.0) * ((1.0 + (i & 7) / 8.0) * 2.0 ** (((i >> 3) & 15) - 7) if i & 120 else (i & 7) * 2.0 ** -9) for i in range(256)])


def e4m3fn_bytes(y):
    return np.clip(np.asarray(y, np.float64), -448.0, 448.0).astype(np.float32).astype(ml_dtypes.float8_e4m3fn).view(np.uint8)


def e4m3fn_values(b):
    return E4M3FN[b]


N, D, M, V = 512, 1024, 2048, 2048


def row_logsumexp(x):
    top = np.max(x, axis=-1, keepdims=True)
    return top + np.log(np.sum(np.exp(x - top), axis=-1, keepdims=True))


def row_softmax(x):
    top = np.max(x, axis=-1, keepdims=True)
    ex = np.exp(x - top)
    return ex / np.sum(ex, axis=-1, keepdims=True)


def sigmoid(v):
    return 1.0 / (1.0 + np.exp(-v))


def draw0():
    s, t = mx_kscale(D), mx_kscale(M)
    h = bf(np.random.standard_normal((N, D)) * s)
    keys = np.random.standard_normal((M, D)) * (32.0 / np.sqrt(D)) / s
    kb = bf(np.random.standard_normal(M))
    g = bf(np.random.standard_normal(M) * t)
    val = np.random.standard_normal((M, V)) * (np.sqrt(M) / 45.0) / t[:, None]
    w_lm = np.random.standard_normal((D, V)) / np.sqrt(D) / s[:, None]
    keys_words, keys_scales = pack_weight(keys.T, "e4m3")
    val_words, val_scales = pack_weight(val, "e4m3")
    w_lm_words, w_lm_scales = pack_weight(w_lm, "e4m3")
    return {
        "h": h,
        "keys_words": keys_words,
        "keys_scales": keys_scales,
        "kb": kb,
        "g": g,
        "val_words": val_words,
        "val_scales": val_scales,
        "w_lm_words": w_lm_words,
        "w_lm_scales": w_lm_scales,
    }


def core(h, keys_words, keys_scales, kb, g, val_words, val_scales, w_lm_words, w_lm_scales):
    vocab = w_lm_words.shape[2]
    hq = mxq(f64(h), 1, "e4m3")

    e = (hq @ unpack_weight(keys_words, keys_scales, "e4m3")) / 20.0 + f64(kb)[None, :]

    l = row_logsumexp(e)
    w = np.exp(e - l)

    a = 8.0 * w * f64(g)[None, :]

    knn = mxq(a, 1, "e4m3") @ unpack_weight(val_words, val_scales, "e4m3")

    z = hq @ unpack_weight(w_lm_words, w_lm_scales, "e4m3")
    p_lm = row_softmax(z)

    lam = sigmoid(4.0 * (l - np.mean(l)))

    return lam * knn + (1.0 - lam) * (vocab * p_lm - 1.0)


def setup_inputs():
    drawn = draw0()
    full = np.asarray(drawn['h']).astype(np.float64)
    scale = (np.abs(full).reshape(512, 8, 128).max(axis=(2,)) / 448.0).astype(np.float32)
    given = {}
    for key, value in drawn.items():
        if key == 'h':
            given['h_bytes'] = e4m3fn_bytes(full / np.repeat(scale.astype(np.float64), 128, axis=1))
            given['h_scale'] = scale
        else:
            given[key] = value
    return given


def reference(h_bytes, h_scale, keys_words, keys_scales, kb, g, val_words, val_scales, w_lm_words, w_lm_scales):
    return core(e4m3fn_values(h_bytes) * np.repeat(h_scale.astype(np.float64), 128, axis=1), keys_words, keys_scales, kb, g, val_words, val_scales, w_lm_words, w_lm_scales)

@@ -1,0 +1,387 @@
+from contextlib import ExitStack
+
+import concourse.mybir as mybir
+from concourse.masks import make_identity
+
+F32 = mybir.dt.float32
+BF16 = mybir.dt.bfloat16
+U32 = mybir.dt.uint32
+I32 = mybir.dt.int32
+U8 = mybir.dt.uint8
+FP8 = mybir.dt.float8_e4m3fn
+FP8X4 = mybir.dt.float8_e4m3fn_x4
+ALU = mybir.AluOpType
+ACT = mybir.ActivationFunctionType
+AX = mybir.AxisListType
+
+P = 128
+N, D, M, V = 512, 1024, 2048, 2048
+TILES = N // P
+CHUNK = 512
+NC = V // CHUNK
+FLOPS = 2 * N * D * M + 2 * N * M * V + 2 * N * D * V
+
+ORDER = """
+identb spread.0 spread.1 spread.2 widen.0.4.s widen.0.5.s widen.0.6.s widen.0.7.s widen.0.0.v widen.0.1.v widen.0.2.v widen.0.3.v turn_h.0
+copy_h.0.0.v keep_kb.0 keep_kb.1 copy_h.0.1.s keep_kb.2 quant_h.0.0 quant_h.0.1 E.0.0 widen.1.1.s widen.1.3.s widen.1.5.s widen.1.7.s
+widen.2.0.s widen.2.1.s widen.2.2.s widen.2.3.s widen.2.4.s widen.2.5.s widen.2.6.s widen.2.7.s spread.3 widen.1.0.v widen.1.2.v widen.1.4.v
+widen.1.6.v turn_h.1 E.0.1 copy_h.1.0.s b.0.0 quant_h.1.0 b.0.1 turn_h.2 E.0.2 copy_h.1.1.s quant_h.1.1 E.0.3 copy_h.2.0.s keep_kb.3 b.0.2
+b.0.3 copy_h.2.1.s E.1.0 quant_h.2.0 E.1.1 E.1.2 E.1.3 quant_h.2.1 widen.3.0.s widen.3.1.s widen.3.2.s widen.3.3.s widen.3.4.s widen.3.5.s
+widen.3.6.s widen.3.7.s turn_h.3 b.1.0 b.1.1 b.1.2 copy_h.3.0.s copy_h.3.1.s E.2.0 E.2.1 E.2.2 E.2.3 b.1.3 quant_h.3.0 c.0 c.1 quant_h.3.1
+E.3.0 E.3.1 m.0 x.0 Z.0.0 zc.0.0 b.2.0 b.2.1 Z.0.1 b.2.2 zc.0.1 Z.0.2 zc.0.2 Z.0.3 zc.0.3 b.2.3 m.1 x.1 g8 b.3.0 E.3.2 E.3.3 c.2 b.3.1 b.3.2
+zm.0 r.0 b.3.3 r.1 a.0.0 a.0.1 y.0.0 y.0.1 y.0.2 m.2 Z.1.0 Z.1.1 z.1.0 Z.1.2 z.1.1 A.0.0 z.1.2 A.0.1 Z.1.3 k.0.0 y.0.3 q.0.0 c.3 m.3 k.0.1
+q.0.1 z.1.3 x.2 x.3 a.1.0 K.0.0 s.1 a.1.1 l1 y.1.0 y.1.1 K.0.1 K.0.2 y.1.2 y.1.3 r.2 r.3 l2 l3 l4 l5 A.1.0 k.1.0 A.1.1 k.1.1 q.1.0 l6 l7
+q.1.1 K.0.3 K.1.0 K.1.1 K.1.2 l8 u.0.0 u.0.1 u.0.2 K.1.3 a.2.0 u.0.3 u.1.0 u.1.1 u.1.2 S.0.2 a.2.1 A.2.0 R.0.2 A.2.1 a.3.0 a.3.1 A.3.0
+l10.0.2 k.2.0 v.0.0.2 q.2.0 k.2.1 q.2.1 A.3.1 u.1.3 Z.2.0 Z.2.1 Z.2.2 Z.2.3 k.3.0 k.3.1 z.2.0 z.2.1 z.2.2 z.2.3 s.2 y.2.0 y.2.1 v.0.2.4
+Z.3.0 z.3.0 y.2.2 y.2.3 Z.3.1 Z.3.2 z.3.1 z.3.2 Z.3.3 z.3.3 s.3 q.3.0 q.3.1 K.2.0 u.2.0 v.1.0.2 v.1.2.4 y.3.0 K.2.1 K.2.2 y.3.1 y.3.2 y.3.3
+S.2.4 K.2.3 K.3.0 K.3.1 K.3.2 K.3.3 R.2.4 l10.2.4 u.2.1 u.2.2 u.2.3 v.2.0.2 u.3.0 u.3.1 u.3.2 u.3.3 v.2.2.4 v.3.0.2 v.3.2.3 v.3.3.4
+"""
+
+
+def tile_gatedmemoryattentionlmhead_kernel(
+    tc, h_bytes, h_scale, keys_words, keys_scales, kb, g, val_words, val_scales, w_lm_words, w_lm_scales, out
+):
+    nc = tc.nc
+    with ExitStack() as ctx:
+        keep = ctx.enter_context(tc.tile_pool(name="keep", bufs=1))
+        work = ctx.enter_context(tc.tile_pool(name="work", bufs=2))
+        psum = ctx.enter_context(tc.psum_pool(name="psum", bufs=8))
+        ctx.enter_context(tc.manual_schedule())
+
+        def bank():
+            b = psum.tile([P, CHUNK], F32, name="bank")
+            return b
+
+        def quads(b):
+            return b[:].rearrange("p (q n) -> p q n", q=4)
+
+        hb = keep.tile([P, TILES, D], U8, name="hb", align_bytes=64)
+        hs = keep.tile([P, TILES * 8], F32, name="hs")
+        rows = keep.tile([P, CHUNK], BF16, name="rows")
+        ident = keep.tile([P, P], F32, name="ident")
+        identb = keep.tile([P, P], BF16, name="identb")
+        root = keep.tile([P, 1], F32, name="root")
+        ones = keep.tile([P, P], F32, name="ones")
+        warm = keep.tile([P, 1], F32, name="warm")
+        kplane = keep.tile([P, M], U8, name="kplane", align_bytes=64)
+        wplane = keep.tile([P, V], U8, name="wplane", align_bytes=64)
+        vplane = keep.tile([P, V], U8, name="vplane", align_bytes=64)
+        kw = [keep.tile([P, 2, CHUNK], U32, name=f"kw{c}", align_bytes=64) for c in range(NC)]
+        ww = [keep.tile([P, 2, CHUNK], U32, name=f"ww{c}", align_bytes=64) for c in range(NC)]
+        vw = [keep.tile([P, 4, CHUNK], U32, name=f"vw{c}", align_bytes=64) for c in range(NC)]
+        kbb = keep.tile([P, M], BF16, name="kbb")
+        gb = keep.tile([P, M], BF16, name="gb")
+        g8p = keep.tile([P, 2, NC * 128, 2], BF16, name="g8p")
+        hq = [keep.tile([P, 2, P], U32, name=f"hq{i}", align_bytes=64) for i in range(TILES)]
+        hqs = [keep.tile([P, 2, P], U8, name=f"hqs{i}", align_bytes=64) for i in range(TILES)]
+        cmx = keep.tile([P, TILES], F32, name="cmx")
+        ncm = [cmx[:, i : i + 1] for i in range(TILES)]
+        sums = keep.tile([P, TILES], F32, name="sums")
+        rs = keep.tile([P, TILES], F32, name="rs")
+        nz = keep.tile([P, TILES * NC], F32, name="nz")
+        nzm = keep.tile([P, TILES], F32, name="nzm")
+        zs = keep.tile([P, TILES * NC], F32, name="zs")
+        sz = keep.tile([P, TILES], F32, name="sz")
+        rsz = keep.tile([P, TILES], F32, name="rsz")
+        st = {k: keep.tile([P, w], F32, name=k) for k, w in (("p4", 1), ("junk4", 4), ("y", 1), ("gp", 1), ("ms", 1), ("r2", 4), ("r4", 4), ("qe", 4), ("q", 4), ("lam", 4), ("c0", 4), ("c1", 4))}
+        junk = keep.tile([P, P], F32, name="junk")
+        e_sb, e_b, ex, prob, a_bf, a_w, aq, aqs, o_sb = {}, {}, {}, {}, {}, {}, {}, {}, {}
+        eb, zb, kb_, ab = {}, {}, {}, {}
+        hw, hg, hbk, z_b = {}, {}, {}, {}
+
+        h_rows = h_bytes.rearrange("(p i) k -> p i k", i=TILES)
+        out_rows = out.rearrange("(p i) n -> p i n", i=TILES)
+
+        def words(w):
+            return w.rearrange("g p n t -> p g (n t)").bitcast(I32)
+
+        def load_words(tiles, w, c):
+            nc.sync.dma_start(out=tiles[c][:].bitcast(I32), in_=words(w)[:, :, c * CHUNK : (c + 1) * CHUNK])
+
+        def load_scales(plane, scales, groups, eng):
+            for q in range(4):
+                eng.dma_start(
+                    out=plane[32 * q : 32 * q + 4 * groups, :].bitcast(I32),
+                    in_=scales.bitcast(I32)[:, 4 * q : 4 * q + 4, :],
+                )
+
+        nc.vector.memset(rows[:], 0.0)
+        nc.vector.memset(kplane[:].bitcast(I32), 0)
+        nc.vector.memset(warm[:], 0.0)
+        nc.sync.dma_start(out=hb[:, 0, :], in_=h_rows[:, 0, :])
+        nc.scalar.dma_start(out=hs[:], in_=h_scale.rearrange("(p i) j -> p (i j)", i=TILES))
+        nc.sync.dma_start(out=rows[0:4, :], in_=kb.rearrange("(c n) -> c n", c=NC))
+        load_words(kw, keys_words, 0)
+        load_scales(kplane, keys_scales, 2, nc.scalar)
+        nc.sync.dma_start(out=hb[:, 1:TILES, :], in_=h_rows[:, 1:TILES, :])
+        nc.scalar.activation(out=warm[:], in_=warm[:], func=ACT.Exp)
+        make_identity(nc, ident[:])
+        nc.gpsimd.memset(wplane[:].bitcast(I32), 0)
+        nc.gpsimd.memset(vplane[:].bitcast(I32), 0)
+        nc.gpsimd.memset(root[:], 1.0 / 128.0)
+        nc.gpsimd.memset(ones[:], 1.0)
+        for c in range(1, NC):
+            load_words(kw, keys_words, c)
+        load_scales(wplane, w_lm_scales, 2, nc.sync)
+        load_scales(vplane, val_scales, 4, nc.sync)
+        for c in range(NC):
+            load_words(ww, w_lm_words, c)
+        nc.sync.dma_start(out=gb[:], in_=g.partition_broadcast(P))
+        for c in range(NC):
+            load_words(vw, val_words, c)
+
+        def identb_():
+            nc.vector.tensor_copy(out=identb[:], in_=ident[:])
+
+        def spread(c):
+            b = bank()
+            ab[("row", c)] = b
+            nc.tensor.matmul(b[:], lhsT=identb[:, c : c + 1].to_broadcast([P, P]), rhs=rows[:], start=True, stop=True)
+
+        def keep_kb(c):
+            nc.scalar.copy(out=kbb[:, c * CHUNK : (c + 1) * CHUNK], in_=ab[("row", c)][:])
+
+        def g8():
+            nc.gpsimd.tensor_scalar(
+                out=g8p[:], in0=gb[:].rearrange("p (w u e) -> p u w e", u=2, e=2), scalar1=8.0, scalar2=0.0, op0=ALU.mult, op1=ALU.add
+            )
+
+        def widen(i, b, eng):
+            if i not in hw:
+                hw[i] = work.tile([P, D], BF16, name="hw", align_bytes=64, bufs=2)
+            o, x, s = hw[i][:, P * b : P * b + P], hb[:, i, P * b : P * b + P].bitcast(FP8), hs[:, 8 * i + b : 8 * i + b + 1]
+            if eng == "v":
+                nc.vector.tensor_scalar(out=o, in0=x, scalar1=s, scalar2=None, op0=ALU.mult)
+            else:
+                nc.scalar.activation(out=o, in_=x, func=ACT.Copy, scale=s)
+
+        def turn_h(i):
+            hbk[i] = bank()
+            w = hw[i][:].bitcast(F32)
+            for gu in range(4):
+                gg, u = gu // 2, gu % 2
+                nc.tensor.transpose(quads(hbk[i])[:, gu, :], w[:, 256 * gg + u : 256 * (gg + 1) : 2], ident[:])
+
+        def copy_h(i, gg, eng):
+            if i not in hg:
+                hg[i] = work.tile([P, 2, 4 * P], BF16, name="hg", align_bytes=64, bufs=2)
+            o = hg[i][:, gg, :].bitcast(F32).rearrange("p (n u) -> p n u", u=2)
+            x = quads(hbk[i])[:, 2 * gg : 2 * gg + 2, :].rearrange("p u n -> p n u")
+            if eng == "v":
+                nc.vector.tensor_copy(out=o, in_=x)
+            else:
+                nc.scalar.copy(out=o, in_=x)
+
+        def quant_h(i, gg):
+            nc.vector.quantize_mx(out=hq[i][:, gg, :].bitcast(FP8X4), scales=hqs[i][:, gg, :], in_=hg[i][:, gg, :])
+
+        def product(b, i, codes, scales, groups, w, plane, c):
+            for gg in range(groups):
+                nc.tensor.matmul_mx(
+                    out=b[:],
+                    lhsT=codes[i][:, gg, :].bitcast(FP8X4),
+                    lhsT_scale=scales[i][:, gg, :],
+                    rhs=w[c][:, gg, :].bitcast(FP8X4),
+                    rhs_scale=plane[4 * gg : P, c * CHUNK : (c + 1) * CHUNK],
+                    start=(gg == 0),
+                    stop=(gg == groups - 1),
+                )
+
+        def E(i, c):
+            eb[i, c] = bank()
+            product(eb[i, c], i, hq, hqs, 2, kw, kplane, c)
+
+        def b(i, c):
+            if i not in e_sb:
+                e_sb[i] = work.tile([P, NC, CHUNK], F32, name="e_sb", bufs=3)
+            nc.vector.scalar_tensor_tensor(
+                out=e_sb[i][:, c, :], in0=eb[i, c][:], scalar=1.0 / 20.0, in1=kbb[:, c * CHUNK : (c + 1) * CHUNK], op0=ALU.mult, op1=ALU.add
+            )
+
+        def c(i):
+            e_b[i] = work.tile([P, M], BF16, name="e_b", bufs=2)
+            nc.gpsimd.tensor_scalar(
+                out=e_b[i][:], in0=e_sb[i][:].rearrange("p c n -> p (c n)"), scalar1=1.0, scalar2=0.0, op0=ALU.mult, op1=ALU.add
+            )
+
+        def cs(i):
+            e_b[i] = work.tile([P, M], BF16, name="e_b", bufs=2)
+            nc.scalar.copy(out=e_b[i][:], in_=e_sb[i][:].rearrange("p c n -> p (c n)"))
+
+        def m(i):
+            nc.vector.tensor_scalar(
+                out=e_b[i][:], in0=e_b[i][:], scalar1=-1.0, scalar2=None, op0=ALU.mult, op1=ALU.min, accum_out=ncm[i]
+            )
+
+        def mf(i):
+            nc.vector.tensor_reduce(out=ncm[i], in_=e_sb[i][:].rearrange("p c n -> p (c n)"), axis=AX.X, op=ALU.max, negate=True)
+
+        def x(i):
+            ex[i] = work.tile([P, 2, NC * 128, 2], F32, name="ex", bufs=3)
+            nc.scalar.activation(
+                out=ex[i][:],
+                in_=e_sb[i][:].rearrange("p c (w u e) -> p u (c w) e", u=2, e=2),
+                func=ACT.Exp,
+                bias=ncm[i],
+                accum_out=sums[:, i : i + 1],
+            )
+
+        def r(i):
+            nc.vector.reciprocal(out=rs[:, i : i + 1], in_=sums[:, i : i + 1])
+
+        def a(i, f):
+            if i not in a_bf:
+                a_bf[i] = work.tile([P, 2, NC * 256], BF16, name="a_bf", align_bytes=64, bufs=2)
+            s = slice(f * 512, f * 512 + 512)
+            nc.vector.scalar_tensor_tensor(
+                out=a_bf[i][:, :, s],
+                in0=ex[i][:].rearrange("p u w e -> p u (w e)")[:, :, s],
+                scalar=rs[:, i : i + 1],
+                in1=g8p[:].rearrange("p u w e -> p u (w e)")[:, :, s],
+                op0=ALU.mult,
+                op1=ALU.mult,
+            )
+
+        def zc(i, c):
+            if i not in z_b:
+                z_b[i] = work.tile([P, NC, CHUNK], BF16, name="z_b", bufs=1)
+            nc.scalar.copy(out=z_b[i][:, c, :], in_=zb[i, c][:])
+
+        def zm(i):
+            zz = z_b[i][:].rearrange("p c n -> p (c n)")
+            nc.vector.tensor_scalar(out=zz, in0=zz, scalar1=-1.0, scalar2=None, op0=ALU.mult, op1=ALU.min, accum_out=nzm[:, i : i + 1])
+
+        def A(i, f):
+            ab[i, f] = bank()
+            w = a_bf[i][:].rearrange("p u w -> p (u w)").bitcast(F32)
+            for ju in range(4):
+                j, u = 2 * f + ju // 2, ju % 2
+                nc.tensor.transpose(quads(ab[i, f])[:, ju, :], w[:, 512 * u + 128 * j : 512 * u + 128 * j + 128], ident[:])
+
+        def k(i, f, eng="s"):
+            if i not in a_w:
+                a_w[i] = work.tile([P, 4, 4 * P], BF16, name="a_w", align_bytes=64, bufs=2)
+            o = a_w[i][:, 2 * f : 2 * f + 2, :].rearrange("p j k -> p (j k)").bitcast(F32).rearrange("p (j n u) -> p j n u", j=2, u=2)
+            xx = ab[i, f][:].rearrange("p (j u n) -> p j n u", j=2, u=2)
+            if eng == "s":
+                nc.scalar.copy(out=o, in_=xx)
+            else:
+                nc.vector.tensor_copy(out=o, in_=xx)
+
+        def q(i, f):
+            if i not in aq:
+                aq[i] = work.tile([P, 4, P], U32, name="aq", align_bytes=64, bufs=4)
+                aqs[i] = work.tile([P, 4, P], U8, name="aqs", align_bytes=64, bufs=4)
+            nc.vector.quantize_mx(
+                out=aq[i][:, 2 * f : 2 * f + 2, :].rearrange("p j n -> p (j n)").bitcast(FP8X4),
+                scales=aqs[i][:, 2 * f : 2 * f + 2, :].rearrange("p j n -> p (j n)"),
+                in_=a_w[i][:, 2 * f : 2 * f + 2, :].rearrange("p j k -> p (j k)"),
+            )
+
+        def Z(i, c):
+            zb[i, c] = bank()
+            product(zb[i, c], i, hq, hqs, 2, ww, wplane, c)
+
+        def z(i, c):
+            nc.vector.tensor_reduce(out=nz[:, NC * i + c : NC * i + c + 1], in_=zb[i, c][:], axis=AX.X, op=ALU.max, negate=True)
+
+        def s(i):
+            nc.vector.tensor_reduce(out=nzm[:, i : i + 1], in_=nz[:, NC * i : NC * i + NC], axis=AX.X, op=ALU.min)
+
+        def y(i, c):
+            if i not in prob:
+                prob[i] = work.tile([P, NC, CHUNK], F32, name="prob", bufs=4)
+            nc.scalar.activation(
+                out=prob[i][:, c, :], in_=zb[i, c][:], func=ACT.Exp, bias=nzm[:, i : i + 1], accum_out=zs[:, NC * i + c : NC * i + c + 1]
+            )
+
+        def l1():
+            nc.vector.tensor_scalar(out=st["junk4"][:], in0=sums[:], scalar1=1.0, scalar2=None, op0=ALU.mult, op1=ALU.mult, accum_out=st["p4"][:])
+            nc.gpsimd.tensor_tensor(out=st["y"][:], in0=st["p4"][:], in1=root[:], op=ALU.pow)
+
+        def l2():
+            nc.gpsimd.tensor_tensor(out=st["r2"][:], in0=rs[:], in1=rs[:], op=ALU.mult)
+            nc.gpsimd.tensor_tensor(out=st["r4"][:], in0=st["r2"][:], in1=st["r2"][:], op=ALU.mult)
+
+        def l3():
+            ab["gate"] = bank()
+            nc.tensor.matmul(ab["gate"][:, P : P + TILES], lhsT=ones[:], rhs=cmx[:], start=True, stop=True)
+            nc.tensor.transpose(ab["gate"][:, 0:P], st["y"][:].to_broadcast([P, P]), ident[:])
+
+        def l4():
+            nc.vector.tensor_scalar(
+                out=st["junk4"][:], in0=ab["gate"][:, P : P + TILES], scalar1=-4.0 / N, scalar2=None, op0=ALU.mult, op1=ALU.add, accum_out=st["ms"][:]
+            )
+            nc.vector.tensor_scalar(out=junk[:], in0=ab["gate"][:, 0:P], scalar1=1.0, scalar2=None, op0=ALU.mult, op1=ALU.mult, accum_out=st["gp"][:])
+            nc.scalar.activation(out=st["qe"][:], in_=cmx[:], func=ACT.Exp, scale=4.0, bias=st["ms"][:])
+
+        def l5():
+            nc.vector.tensor_tensor(out=st["q"][:], in0=st["qe"][:], in1=st["r4"][:], op=ALU.mult)
+
+        def l6():
+            nc.vector.tensor_scalar(out=st["q"][:], in0=st["q"][:], scalar1=st["gp"][:], scalar2=1.0, op0=ALU.mult, op1=ALU.add)
+
+        def l7():
+            nc.vector.reciprocal(out=st["lam"][:], in_=st["q"][:])
+
+        def l8():
+            nc.vector.tensor_scalar(out=st["c0"][:], in0=st["lam"][:], scalar1=-1.0, scalar2=None, op0=ALU.add)
+
+        def S(lo, hi):
+            nc.vector.tensor_reduce(
+                out=sz[:, lo:hi], in_=zs[:, NC * lo : NC * hi].rearrange("p (i c) -> p i c", c=NC), axis=AX.X, op=ALU.add
+            )
+
+        def R(lo, hi):
+            nc.vector.reciprocal(out=rsz[:, lo:hi], in_=sz[:, lo:hi])
+
+        def l10(lo, hi):
+            nc.vector.scalar_tensor_tensor(
+                out=st["c1"][:, lo:hi], in0=st["c0"][:, lo:hi], scalar=-float(V), in1=rsz[:, lo:hi], op0=ALU.mult, op1=ALU.mult
+            )
+
+        def K(i, c):
+            kb_[i, c] = bank()
+            product(kb_[i, c], i, aq, aqs, 4, vw, vplane, c)
+
+        def T(i, lo=0, hi=NC, eng="g"):
+            t = prob[i][:, lo:hi, :].rearrange("p c n -> p (c n)")
+            if eng == "g":
+                nc.gpsimd.tensor_scalar(out=t, in0=t, scalar1=st["c1"][:, i : i + 1], scalar2=st["c0"][:, i : i + 1], op0=ALU.mult, op1=ALU.add)
+            else:
+                nc.scalar.activation(out=t, in_=t, func=ACT.Identity, scale=st["c1"][:, i : i + 1], bias=st["c0"][:, i : i + 1])
+
+        def f(i, c):
+            if i not in o_sb:
+                o_sb[i] = work.tile([P, NC, CHUNK], F32, name="o_sb", bufs=2)
+            nc.vector.scalar_tensor_tensor(
+                out=o_sb[i][:, c, :], in0=kb_[i, c][:], scalar=st["lam"][:, i : i + 1], in1=prob[i][:, c, :], op0=ALU.mult, op1=ALU.add
+            )
+            nc.sync.dma_start(out=out_rows[:, i, c * CHUNK : (c + 1) * CHUNK], in_=o_sb[i][:, c, :])
+
+        def u(i, c):
+            if i not in o_sb:
+                o_sb[i] = work.tile([P, NC, CHUNK], F32, name="o_sb", bufs=2)
+            nc.scalar.activation(
+                out=o_sb[i][:, c, :], in_=kb_[i, c][:], func=ACT.Identity, scale=st["lam"][:, i : i + 1], bias=st["c0"][:, i : i + 1]
+            )
+
+        def v(i, lo, hi):
+            nc.vector.scalar_tensor_tensor(
+                out=o_sb[i][:, lo:hi, :].rearrange("p c n -> p (c n)"),
+                in0=prob[i][:, lo:hi, :].rearrange("p c n -> p (c n)"),
+                scalar=st["c1"][:, i : i + 1],
+                in1=o_sb[i][:, lo:hi, :].rearrange("p c n -> p (c n)"),
+                op0=ALU.mult,
+                op1=ALU.add,
+            )
+            nc.sync.dma_start(out=out_rows[:, i, lo * CHUNK : hi * CHUNK], in_=o_sb[i][:, lo:hi, :].rearrange("p c n -> p (c n)"))
+
+        steps = {
+            "g8": g8, "identb": identb_, "spread": spread, "keep_kb": keep_kb, "widen": widen, "turn_h": turn_h, "copy_h": copy_h, "quant_h": quant_h,
+            "E": E, "b": b, "c": c, "u": u, "v": v, "cs": cs, "m": m, "mf": mf, "x": x, "r": r, "a": a, "A": A, "k": k, "q": q, "Z": Z, "z": z, "s": s, "y": y, "S": S,
+            "zc": zc, "zm": zm, "l1": l1, "l2": l2, "l3": l3, "l4": l4, "l5": l5, "l6": l6, "l7": l7, "l8": l8, "l10": l10, "R": R, "K": K, "T": T, "f": f,
+        }
+        for token in ORDER.split():
+            parts = token.split(".")
+            steps[parts[0]](*[int(v) if v not in ("v", "s", "g") else v for v in parts[1:]])

@@ -22,19 +22,20 @@ NC = V // CHUNK
 FLOPS = 2 * N * D * M + 2 * N * M * V + 2 * N * D * V
 
 ORDER = """
-identb spread.0 spread.1 spread.2 widen.0.4.s widen.0.5.s widen.0.6.s widen.0.7.s widen.0.0.v widen.0.1.v widen.0.2.v widen.0.3.v turn_h.0
-copy_h.0.0.v keep_kb.0 keep_kb.1 copy_h.0.1.s keep_kb.2 quant_h.0.0 quant_h.0.1 E.0.0 widen.1.1.s widen.1.3.s widen.1.5.s widen.1.7.s
-widen.2.0.s widen.2.1.s widen.2.2.s widen.2.3.s widen.2.4.s widen.2.5.s widen.2.6.s widen.2.7.s spread.3 widen.1.0.v widen.1.2.v widen.1.4.v
-widen.1.6.v turn_h.1 E.0.1 copy_h.1.0.s b.0.0 quant_h.1.0 b.0.1 turn_h.2 E.0.2 copy_h.1.1.s quant_h.1.1 E.0.3 copy_h.2.0.s keep_kb.3 b.0.2
-b.0.3 copy_h.2.1.s E.1.0 quant_h.2.0 E.1.1 E.1.2 E.1.3 quant_h.2.1 widen.3.0.s widen.3.1.s widen.3.2.s widen.3.3.s widen.3.4.s widen.3.5.s
-widen.3.6.s widen.3.7.s turn_h.3 b.1.0 b.1.1 b.1.2 copy_h.3.0.s copy_h.3.1.s E.2.0 E.2.1 E.2.2 E.2.3 b.1.3 quant_h.3.0 c.0 c.1 quant_h.3.1
-E.3.0 E.3.1 m.0 x.0 Z.0.0 zc.0.0 b.2.0 b.2.1 Z.0.1 b.2.2 zc.0.1 Z.0.2 zc.0.2 Z.0.3 zc.0.3 b.2.3 m.1 x.1 g8 b.3.0 E.3.2 E.3.3 c.2 b.3.1 b.3.2
-zm.0 r.0 b.3.3 r.1 a.0.0 a.0.1 y.0.0 y.0.1 y.0.2 m.2 Z.1.0 Z.1.1 z.1.0 Z.1.2 z.1.1 A.0.0 z.1.2 A.0.1 Z.1.3 k.0.0 y.0.3 q.0.0 c.3 m.3 k.0.1
-q.0.1 z.1.3 x.2 x.3 a.1.0 K.0.0 s.1 a.1.1 l1 y.1.0 y.1.1 K.0.1 K.0.2 y.1.2 y.1.3 r.2 r.3 l2 l3 l4 l5 A.1.0 k.1.0 A.1.1 k.1.1 q.1.0 l6 l7
-q.1.1 K.0.3 K.1.0 K.1.1 K.1.2 l8 u.0.0 u.0.1 u.0.2 K.1.3 a.2.0 u.0.3 u.1.0 u.1.1 u.1.2 S.0.2 a.2.1 A.2.0 R.0.2 A.2.1 a.3.0 a.3.1 A.3.0
-l10.0.2 k.2.0 v.0.0.2 q.2.0 k.2.1 q.2.1 A.3.1 u.1.3 Z.2.0 Z.2.1 Z.2.2 Z.2.3 k.3.0 k.3.1 z.2.0 z.2.1 z.2.2 z.2.3 s.2 y.2.0 y.2.1 v.0.2.4
-Z.3.0 z.3.0 y.2.2 y.2.3 Z.3.1 Z.3.2 z.3.1 z.3.2 Z.3.3 z.3.3 s.3 q.3.0 q.3.1 K.2.0 u.2.0 v.1.0.2 v.1.2.4 y.3.0 K.2.1 K.2.2 y.3.1 y.3.2 y.3.3
-S.2.4 K.2.3 K.3.0 K.3.1 K.3.2 K.3.3 R.2.4 l10.2.4 u.2.1 u.2.2 u.2.3 v.2.0.2 u.3.0 u.3.1 u.3.2 u.3.3 v.2.2.4 v.3.0.2 v.3.2.3 v.3.3.4
+widen.0.0.v widen.0.1.v widen.0.4.s widen.0.5.s widen.0.6.s widen.0.7.s widen.0.2.v identb spread.0 spread.1 widen.0.3.v turn_h.0 spread.2
+copy_h.0.0.v quant_h.0.0 keep_kb.0 keep_kb.1 spread.3 copy_h.0.1.s quant_h.0.1 E.0.0 E.0.1 keep_kb.2 widen.1.1.s widen.1.3.s widen.1.5.s
+widen.1.7.s widen.2.0.s widen.2.1.s widen.2.2.s widen.2.3.s widen.1.0.v widen.1.2.v widen.1.4.v widen.1.6.v turn_h.1 b.0.0 b.0.1 E.0.2
+copy_h.1.0.s quant_h.1.0 copy_h.1.1.s quant_h.1.1 keep_kb.3 widen.2.4.s widen.2.5.s widen.2.6.s widen.2.7.s widen.3.0.s widen.3.1.s b.0.2
+E.0.3 E.1.0 b.0.3 turn_h.2 widen.3.2.s widen.3.3.s widen.3.4.s widen.3.5.s b.1.0 ma.0 E.1.1 E.1.2 E.1.3 copy_h.2.0.s copy_h.2.1.s
+quant_h.2.0 g8 widen.3.6.s widen.3.7.s quant_h.2.1 E.2.0 E.2.1 E.2.2 E.2.3 b.1.1 mb.0 x.0 b.1.2 b.1.3 b.2.0 turn_h.3 copy_h.3.0.s
+copy_h.3.1.s Z.0.0 Z.0.1 ma.1 b.2.1 mb.1 Z.0.2 quant_h.3.0 Z.0.3 quant_h.3.1 r.0 zc.0.0 zc.0.1 E.3.0 b.2.2 E.3.1 zc.0.2 E.3.2 E.3.3 a.0.0
+b.2.3 zc.0.3 zm.0 x.1 a.0.1 A.0.0 A.0.1 y.0.0 r.1 y.0.1 y.0.2 b.3.0 a.1.0 y.0.3 a.1.1 A.1.0 k.0.0 b.3.1 A.1.1 ma.2 b.3.2 k.0.1 k.1.0 b.3.3
+mb.2 q.0.0 ma.3 Z.1.0 Z.1.1 k.1.1 q.0.1 Z.1.2 Z.1.3 mb.3 x.2 z.1.0 z.1.1 z.1.2 z.1.3 x.3 q.1.0 s.1 y.1.0 K.0.0 K.0.1 K.0.2 K.0.3 l1 r.2 r.3
+l2 l9 y.1.1 q.1.1 l3 K.1.0 K.1.1 K.1.2 Z.2.0 l4 l5 l6 a.2.0 l7 y.1.2 y.1.3 S.0.2 l8 Z.2.1 Z.2.2 Z.2.3 u.0.0 u.0.1 u.0.2 u.0.3 u.1.0 u.1.1
+u.1.2 a.2.1 A.2.0 A.2.1 a.3.0 k.2.0 K.1.3 z.2.0 z.2.1 Z.3.0 Z.3.1 z.2.2 z.2.3 R.0.2 s.2 Z.3.2 Z.3.3 y.2.0 a.3.1 q.2.0 y.2.1 y.2.2 y.2.3
+z.3.0 A.3.0 A.3.1 z.3.1 z.3.2 z.3.3 k.2.1 k.3.0 q.2.1 l10.0.2 K.2.0 s.3 q.3.0 v.0.0.2 v.0.2.4 v.1.0.2 u.1.3 y.3.0 y.3.1 k.3.1 y.3.2 y.3.3
+S.2.4 u.2.0 K.2.1 q.3.1 R.2.4 K.2.2 K.2.3 K.3.0 K.3.1 K.3.2 u.2.1 u.2.2 u.2.3 v.1.2.4 u.3.0 u.3.1 u.3.2 l10.2.4 v.2.0.2 v.2.2.4 K.3.3 u.3.3
+v.3.0.2 v.3.2.3 v.3.3.4
 """
 
 
@@ -122,11 +123,11 @@ def tile_gatedmemoryattentionlmhead_kernel(
         nc.gpsimd.memset(ones[:], 1.0)
         for c in range(1, NC):
             load_words(kw, keys_words, c)
+        nc.sync.dma_start(out=gb[:], in_=g.partition_broadcast(P))
         load_scales(wplane, w_lm_scales, 2, nc.sync)
         load_scales(vplane, val_scales, 4, nc.sync)
         for c in range(NC):
             load_words(ww, w_lm_words, c)
-        nc.sync.dma_start(out=gb[:], in_=g.partition_broadcast(P))
         for c in range(NC):
             load_words(vw, val_words, c)
 
@@ -142,9 +143,7 @@ def tile_gatedmemoryattentionlmhead_kernel(
             nc.scalar.copy(out=kbb[:, c * CHUNK : (c + 1) * CHUNK], in_=ab[("row", c)][:])
 
         def g8():
-            nc.gpsimd.tensor_scalar(
-                out=g8p[:], in0=gb[:].rearrange("p (w u e) -> p u w e", u=2, e=2), scalar1=8.0, scalar2=0.0, op0=ALU.mult, op1=ALU.add
-            )
+            nc.scalar.activation(out=g8p[:], in_=gb[:].rearrange("p (w u e) -> p u w e", u=2, e=2), func=ACT.Copy, scale=8.0)
 
         def widen(i, b, eng):
             if i not in hw:
@@ -212,6 +211,16 @@ def tile_gatedmemoryattentionlmhead_kernel(
             nc.vector.tensor_scalar(
                 out=e_b[i][:], in0=e_b[i][:], scalar1=-1.0, scalar2=None, op0=ALU.mult, op1=ALU.min, accum_out=ncm[i]
             )
+
+        def ma(i):
+            e_b[i] = work.tile([P, M], BF16, name="e_b", bufs=2)
+            nc.vector.tensor_tensor(
+                out=e_b[i][:, 0 : M // 2].rearrange("p (c n) -> p c n", c=2), in0=e_sb[i][:, 0:2, :], in1=e_sb[i][:, 2:4, :], op=ALU.max
+            )
+
+        def mb(i):
+            h = e_b[i][:, 0 : M // 2]
+            nc.vector.tensor_scalar(out=h, in0=h, scalar1=-1.0, scalar2=None, op0=ALU.mult, op1=ALU.min, accum_out=ncm[i])
 
         def mf(i):
             nc.vector.tensor_reduce(out=ncm[i], in_=e_sb[i][:].rearrange("p c n -> p (c n)"), axis=AX.X, op=ALU.max, negate=True)
@@ -300,8 +309,10 @@ def tile_gatedmemoryattentionlmhead_kernel(
             nc.gpsimd.tensor_tensor(out=st["y"][:], in0=st["p4"][:], in1=root[:], op=ALU.pow)
 
         def l2():
-            nc.gpsimd.tensor_tensor(out=st["r2"][:], in0=rs[:], in1=rs[:], op=ALU.mult)
-            nc.gpsimd.tensor_tensor(out=st["r4"][:], in0=st["r2"][:], in1=st["r2"][:], op=ALU.mult)
+            nc.vector.tensor_tensor(out=st["r2"][:], in0=rs[:], in1=rs[:], op=ALU.mult)
+
+        def l9():
+            nc.vector.tensor_tensor(out=st["r4"][:], in0=st["r2"][:], in1=st["r2"][:], op=ALU.mult)
 
         def l3():
             ab["gate"] = bank()
@@ -366,6 +377,22 @@ def tile_gatedmemoryattentionlmhead_kernel(
                 out=o_sb[i][:, c, :], in_=kb_[i, c][:], func=ACT.Identity, scale=st["lam"][:, i : i + 1], bias=st["c0"][:, i : i + 1]
             )
 
+        def w(i, c):
+            if i not in o_sb:
+                o_sb[i] = work.tile([P, NC, CHUNK], F32, name="o_sb", bufs=2)
+            nc.scalar.copy(out=o_sb[i][:, c, :], in_=kb_[i, c][:])
+
+        def gx(i, lo, hi):
+            nc.vector.scalar_tensor_tensor(
+                out=o_sb[i][:, lo:hi, :].rearrange("p c n -> p (c n)"),
+                in0=o_sb[i][:, lo:hi, :].rearrange("p c n -> p (c n)"),
+                scalar=st["lam"][:, i : i + 1],
+                in1=prob[i][:, lo:hi, :].rearrange("p c n -> p (c n)"),
+                op0=ALU.mult,
+                op1=ALU.add,
+            )
+            nc.sync.dma_start(out=out_rows[:, i, lo * CHUNK : hi * CHUNK], in_=o_sb[i][:, lo:hi, :].rearrange("p c n -> p (c n)"))
+
         def v(i, lo, hi):
             nc.vector.scalar_tensor_tensor(
                 out=o_sb[i][:, lo:hi, :].rearrange("p c n -> p (c n)"),
@@ -379,8 +406,8 @@ def tile_gatedmemoryattentionlmhead_kernel(
 
         steps = {
             "g8": g8, "identb": identb_, "spread": spread, "keep_kb": keep_kb, "widen": widen, "turn_h": turn_h, "copy_h": copy_h, "quant_h": quant_h,
-            "E": E, "b": b, "c": c, "u": u, "v": v, "cs": cs, "m": m, "mf": mf, "x": x, "r": r, "a": a, "A": A, "k": k, "q": q, "Z": Z, "z": z, "s": s, "y": y, "S": S,
-            "zc": zc, "zm": zm, "l1": l1, "l2": l2, "l3": l3, "l4": l4, "l5": l5, "l6": l6, "l7": l7, "l8": l8, "l10": l10, "R": R, "K": K, "T": T, "f": f,
+            "E": E, "b": b, "c": c, "u": u, "v": v, "w": w, "gx": gx, "cs": cs, "m": m, "mf": mf, "ma": ma, "mb": mb, "x": x, "r": r, "a": a, "A": A, "k": k, "q": q, "Z": Z, "z": z, "s": s, "y": y, "S": S,
+            "zc": zc, "zm": zm, "l1": l1, "l2": l2, "l3": l3, "l4": l4, "l5": l5, "l6": l6, "l7": l7, "l8": l8, "l9": l9, "l10": l10, "R": R, "K": K, "T": T, "f": f,
         }
         for token in ORDER.split():
             parts = token.split(".")

@@ -22,20 +22,20 @@ NC = V // CHUNK
 FLOPS = 2 * N * D * M + 2 * N * M * V + 2 * N * D * V
 
 ORDER = """
-widen.0.0.v widen.0.1.v widen.0.4.s widen.0.5.s widen.0.6.s widen.0.7.s widen.0.2.v identb spread.0 spread.1 widen.0.3.v turn_h.0 spread.2
-copy_h.0.0.v quant_h.0.0 keep_kb.0 keep_kb.1 spread.3 copy_h.0.1.s quant_h.0.1 E.0.0 E.0.1 keep_kb.2 widen.1.1.s widen.1.3.s widen.1.5.s
-widen.1.7.s widen.2.0.s widen.2.1.s widen.2.2.s widen.2.3.s widen.1.0.v widen.1.2.v widen.1.4.v widen.1.6.v turn_h.1 b.0.0 b.0.1 E.0.2
-copy_h.1.0.s quant_h.1.0 copy_h.1.1.s quant_h.1.1 keep_kb.3 widen.2.4.s widen.2.5.s widen.2.6.s widen.2.7.s widen.3.0.s widen.3.1.s b.0.2
-E.0.3 E.1.0 b.0.3 turn_h.2 widen.3.2.s widen.3.3.s widen.3.4.s widen.3.5.s b.1.0 ma.0 E.1.1 E.1.2 E.1.3 copy_h.2.0.s copy_h.2.1.s
-quant_h.2.0 g8 widen.3.6.s widen.3.7.s quant_h.2.1 E.2.0 E.2.1 E.2.2 E.2.3 b.1.1 mb.0 x.0 b.1.2 b.1.3 b.2.0 turn_h.3 copy_h.3.0.s
-copy_h.3.1.s Z.0.0 Z.0.1 ma.1 b.2.1 mb.1 Z.0.2 quant_h.3.0 Z.0.3 quant_h.3.1 r.0 zc.0.0 zc.0.1 E.3.0 b.2.2 E.3.1 zc.0.2 E.3.2 E.3.3 a.0.0
-b.2.3 zc.0.3 zm.0 x.1 a.0.1 A.0.0 A.0.1 y.0.0 r.1 y.0.1 y.0.2 b.3.0 a.1.0 y.0.3 a.1.1 A.1.0 k.0.0 b.3.1 A.1.1 ma.2 b.3.2 k.0.1 k.1.0 b.3.3
-mb.2 q.0.0 ma.3 Z.1.0 Z.1.1 k.1.1 q.0.1 Z.1.2 Z.1.3 mb.3 x.2 z.1.0 z.1.1 z.1.2 z.1.3 x.3 q.1.0 s.1 y.1.0 K.0.0 K.0.1 K.0.2 K.0.3 l1 r.2 r.3
-l2 l9 y.1.1 q.1.1 l3 K.1.0 K.1.1 K.1.2 Z.2.0 l4 l5 l6 a.2.0 l7 y.1.2 y.1.3 S.0.2 l8 Z.2.1 Z.2.2 Z.2.3 u.0.0 u.0.1 u.0.2 u.0.3 u.1.0 u.1.1
-u.1.2 a.2.1 A.2.0 A.2.1 a.3.0 k.2.0 K.1.3 z.2.0 z.2.1 Z.3.0 Z.3.1 z.2.2 z.2.3 R.0.2 s.2 Z.3.2 Z.3.3 y.2.0 a.3.1 q.2.0 y.2.1 y.2.2 y.2.3
-z.3.0 A.3.0 A.3.1 z.3.1 z.3.2 z.3.3 k.2.1 k.3.0 q.2.1 l10.0.2 K.2.0 s.3 q.3.0 v.0.0.2 v.0.2.4 v.1.0.2 u.1.3 y.3.0 y.3.1 k.3.1 y.3.2 y.3.3
-S.2.4 u.2.0 K.2.1 q.3.1 R.2.4 K.2.2 K.2.3 K.3.0 K.3.1 K.3.2 u.2.1 u.2.2 u.2.3 v.1.2.4 u.3.0 u.3.1 u.3.2 l10.2.4 v.2.0.2 v.2.2.4 K.3.3 u.3.3
-v.3.0.2 v.3.2.3 v.3.3.4
+identb widen.0.4.s widen.0.5.s spread.0 spread.1 spread.2 widen.0.0.v widen.0.1.v widen.0.2.v widen.0.6.s widen.0.7.s keep_kb.0 keep_kb.1
+widen.0.3.v turn_h.0 copy_h.0.0.v copy_h.0.1.s quant_h.0.0 quant_h.0.1 spread.3 spread.4 keep_kb.2 widen.1.0.v widen.1.2.v widen.1.4.v
+spread.5 widen.1.1.s widen.1.3.s widen.1.5.s widen.1.7.s widen.1.6.v E.0.0 keep_g.0 b.0.0 turn_h.1 copy_h.1.0.s keep_kb.3 copy_h.1.1.s E.0.1
+quant_h.1.0 keep_g.1 b.0.1 quant_h.1.1 E.0.2 spread.6 widen.2.0.s widen.2.1.s widen.2.2.s widen.2.3.s widen.2.4.s widen.2.5.s E.0.3
+widen.2.6.s widen.2.7.s b.0.2 E.1.0 b.0.3 b.1.0 E.1.1 widen.3.0.s widen.3.1.s widen.3.2.s ma.0 spread.7 b.1.1 keep_g.2 widen.3.3.s turn_h.2
+copy_h.2.0.s E.1.2 copy_h.2.1.s quant_h.2.0 quant_h.2.1 E.1.3 E.2.0 E.2.1 E.2.2 E.2.3 widen.3.4.s mb.0 widen.3.5.s b.1.2 Z.0.0 keep_g.3
+widen.3.6.s widen.3.7.s b.1.3 b.2.0 Z.0.1 Z.0.2 Z.0.3 b.2.1 b.2.2 x.0 r.0 b.2.3 a.0.0 zc.0.0 zc.0.1 a.0.1 zc.0.2 zc.0.3 turn_h.3 zm.0 A.0.0
+A.0.1 copy_h.3.0.s copy_h.3.1.s quant_h.3.0 quant_h.3.1 E.3.0 E.3.1 k.0.0 k.0.1 y.0.0 y.0.1 y.0.2 y.0.3 ma.1 q.0.0 q.0.1 E.3.2 mb.1 x.1 ma.2
+b.3.0 mb.2 b.3.1 E.3.3 b.3.2 r.1 x.2 K.0.0 w.0.0 K.0.1 w.0.1 K.0.2 w.0.2 K.0.3 w.0.3 b.3.3 a.1.0 a.1.1 A.1.0 A.1.1 Z.1.0 Z.1.1 ma.3 r.2
+k.1.0 Z.1.2 Z.1.3 k.1.1 mb.3 x.3 Z.2.0 Z.2.1 Z.2.2 Z.2.3 z.1.0 z.1.1 z.1.2 z.1.3 z.2.0 s.1 q.1.0 l1 q.1.1 r.3 z.2.1 y.1.0 y.1.1 K.1.0 y.1.2
+y.1.3 l2 z.2.2 z.2.3 l9 l3 K.1.1 l4 s.2 y.2.0 y.2.1 y.2.2 y.2.3 S.0.2 l5 a.2.0 l6 R.0.2 l7 a.2.1 K.1.2 K.1.3 l8 u.1.0 A.2.0 k.2.0 A.2.1
+k.2.1 u.1.1 a.3.0 a.3.1 u.1.2 Z.3.0 Z.3.1 Z.3.2 Z.3.3 l10.0.2 u.1.3 A.3.0 k.3.0 q.2.0 q.2.1 z.3.0 z.3.1 z.3.2 z.3.3 s.3 q.3.0 A.3.1 k.3.1
+K.2.0 T.0 gx.0.0.2 K.2.1 gx.0.2.4 y.3.0 y.3.1 y.3.2 y.3.3 S.2.4 q.3.1 R.2.4 K.2.2 K.2.3 v.1.0.2 l10.2.4 u.2.0 u.2.1 v.1.2.4 v.2.0.2 u.2.2
+u.2.3 v.2.2.4 K.3.0 u.3.0 K.3.1 K.3.2 K.3.3 u.3.1 u.3.2 v.3.0.2 v.3.2.3 u.3.3 v.3.3.4
 """
 
 
@@ -59,11 +59,11 @@ def tile_gatedmemoryattentionlmhead_kernel(
         hb = keep.tile([P, TILES, D], U8, name="hb", align_bytes=64)
         hs = keep.tile([P, TILES * 8], F32, name="hs")
         rows = keep.tile([P, CHUNK], BF16, name="rows")
+        rows_g = keep.tile([P, CHUNK], BF16, name="rows_g")
         ident = keep.tile([P, P], F32, name="ident")
         identb = keep.tile([P, P], BF16, name="identb")
         root = keep.tile([P, 1], F32, name="root")
         ones = keep.tile([P, P], F32, name="ones")
-        warm = keep.tile([P, 1], F32, name="warm")
         kplane = keep.tile([P, M], U8, name="kplane", align_bytes=64)
         wplane = keep.tile([P, V], U8, name="wplane", align_bytes=64)
         vplane = keep.tile([P, V], U8, name="vplane", align_bytes=64)
@@ -71,7 +71,6 @@ def tile_gatedmemoryattentionlmhead_kernel(
         ww = [keep.tile([P, 2, CHUNK], U32, name=f"ww{c}", align_bytes=64) for c in range(NC)]
         vw = [keep.tile([P, 4, CHUNK], U32, name=f"vw{c}", align_bytes=64) for c in range(NC)]
         kbb = keep.tile([P, M], BF16, name="kbb")
-        gb = keep.tile([P, M], BF16, name="gb")
         g8p = keep.tile([P, 2, NC * 128, 2], BF16, name="g8p")
         hq = [keep.tile([P, 2, P], U32, name=f"hq{i}", align_bytes=64) for i in range(TILES)]
         hqs = [keep.tile([P, 2, P], U8, name=f"hqs{i}", align_bytes=64) for i in range(TILES)]
@@ -108,24 +107,24 @@ def tile_gatedmemoryattentionlmhead_kernel(
 
         nc.vector.memset(rows[:], 0.0)
         nc.vector.memset(kplane[:].bitcast(I32), 0)
-        nc.vector.memset(warm[:], 0.0)
+        nc.vector.memset(ones[:], 0.0)
+        nc.vector.memset(rows_g[:], 0.0)
+        nc.vector.memset(wplane[:].bitcast(I32), 0)
+        nc.vector.memset(vplane[:].bitcast(I32), 0)
         nc.sync.dma_start(out=hb[:, 0, :], in_=h_rows[:, 0, :])
         nc.scalar.dma_start(out=hs[:], in_=h_scale.rearrange("(p i) j -> p (i j)", i=TILES))
         nc.sync.dma_start(out=rows[0:4, :], in_=kb.rearrange("(c n) -> c n", c=NC))
         load_words(kw, keys_words, 0)
         load_scales(kplane, keys_scales, 2, nc.scalar)
         nc.sync.dma_start(out=hb[:, 1:TILES, :], in_=h_rows[:, 1:TILES, :])
-        nc.scalar.activation(out=warm[:], in_=warm[:], func=ACT.Exp)
+        nc.scalar.activation(out=ones[:], in_=ones[:], func=ACT.Exp)
         make_identity(nc, ident[:])
-        nc.gpsimd.memset(wplane[:].bitcast(I32), 0)
-        nc.gpsimd.memset(vplane[:].bitcast(I32), 0)
+        nc.gpsimd.dma_start(out=rows_g[0:4, :], in_=g.rearrange("(c n) -> c n", c=NC))
         nc.gpsimd.memset(root[:], 1.0 / 128.0)
-        nc.gpsimd.memset(ones[:], 1.0)
         for c in range(1, NC):
             load_words(kw, keys_words, c)
-        nc.sync.dma_start(out=gb[:], in_=g.partition_broadcast(P))
-        load_scales(wplane, w_lm_scales, 2, nc.sync)
-        load_scales(vplane, val_scales, 4, nc.sync)
+        load_scales(wplane, w_lm_scales, 2, nc.gpsimd)
+        load_scales(vplane, val_scales, 4, nc.gpsimd)
         for c in range(NC):
             load_words(ww, w_lm_words, c)
         for c in range(NC):
@@ -137,13 +136,19 @@ def tile_gatedmemoryattentionlmhead_kernel(
         def spread(c):
             b = bank()
             ab[("row", c)] = b
-            nc.tensor.matmul(b[:], lhsT=identb[:, c : c + 1].to_broadcast([P, P]), rhs=rows[:], start=True, stop=True)
+            r = rows if c < NC else rows_g
+            nc.tensor.matmul(b[:], lhsT=identb[:, c % NC : c % NC + 1].to_broadcast([P, P]), rhs=r[:], start=True, stop=True)
 
         def keep_kb(c):
             nc.scalar.copy(out=kbb[:, c * CHUNK : (c + 1) * CHUNK], in_=ab[("row", c)][:])
 
-        def g8():
-            nc.scalar.activation(out=g8p[:], in_=gb[:].rearrange("p (w u e) -> p u w e", u=2, e=2), func=ACT.Copy, scale=8.0)
+        def keep_g(c):
+            nc.scalar.activation(
+                out=g8p[:, :, c * P : (c + 1) * P, :],
+                in_=ab["row", NC + c][:].rearrange("p (w u e) -> p u w e", u=2, e=2),
+                func=ACT.Copy,
+                scale=8.0,
+            )
 
         def widen(i, b, eng):
             if i not in hw:
@@ -405,7 +410,7 @@ def tile_gatedmemoryattentionlmhead_kernel(
             nc.sync.dma_start(out=out_rows[:, i, lo * CHUNK : hi * CHUNK], in_=o_sb[i][:, lo:hi, :].rearrange("p c n -> p (c n)"))
 
         steps = {
-            "g8": g8, "identb": identb_, "spread": spread, "keep_kb": keep_kb, "widen": widen, "turn_h": turn_h, "copy_h": copy_h, "quant_h": quant_h,
+            "keep_g": keep_g, "identb": identb_, "spread": spread, "keep_kb": keep_kb, "widen": widen, "turn_h": turn_h, "copy_h": copy_h, "quant_h": quant_h,
             "E": E, "b": b, "c": c, "u": u, "v": v, "w": w, "gx": gx, "cs": cs, "m": m, "mf": mf, "ma": ma, "mb": mb, "x": x, "r": r, "a": a, "A": A, "k": k, "q": q, "Z": Z, "z": z, "s": s, "y": y, "S": S,
             "zc": zc, "zm": zm, "l1": l1, "l2": l2, "l3": l3, "l4": l4, "l5": l5, "l6": l6, "l7": l7, "l8": l8, "l9": l9, "l10": l10, "R": R, "K": K, "T": T, "f": f,
         }

@@ -18,24 +18,33 @@ P = 128
 N, D, M, V = 512, 1024, 2048, 2048
 TILES = N // P
 CHUNK = 512
-NC = V // CHUNK
+CHUNKS = V // CHUNK
+BLOCK = 128
+BLOCKS = D // BLOCK
+D_PASSES, M_PASSES = D // 512, M // 512
+PAIR = 2 * P
+
 FLOPS = 2 * N * D * M + 2 * N * M * V + 2 * N * D * V
 
 ORDER = """
-identb widen.0.4.s widen.0.5.s spread.0 spread.1 spread.2 widen.0.0.v widen.0.1.v widen.0.2.v widen.0.6.s widen.0.7.s keep_kb.0 keep_kb.1
-widen.0.3.v turn_h.0 copy_h.0.0.v copy_h.0.1.s quant_h.0.0 quant_h.0.1 spread.3 spread.4 keep_kb.2 widen.1.0.v widen.1.2.v widen.1.4.v
-spread.5 widen.1.1.s widen.1.3.s widen.1.5.s widen.1.7.s widen.1.6.v E.0.0 keep_g.0 b.0.0 turn_h.1 copy_h.1.0.s keep_kb.3 copy_h.1.1.s E.0.1
-quant_h.1.0 keep_g.1 b.0.1 quant_h.1.1 E.0.2 spread.6 widen.2.0.s widen.2.1.s widen.2.2.s widen.2.3.s widen.2.4.s widen.2.5.s E.0.3
-widen.2.6.s widen.2.7.s b.0.2 E.1.0 b.0.3 b.1.0 E.1.1 widen.3.0.s widen.3.1.s widen.3.2.s ma.0 spread.7 b.1.1 keep_g.2 widen.3.3.s turn_h.2
-copy_h.2.0.s E.1.2 copy_h.2.1.s quant_h.2.0 quant_h.2.1 E.1.3 E.2.0 E.2.1 E.2.2 E.2.3 widen.3.4.s mb.0 widen.3.5.s b.1.2 Z.0.0 keep_g.3
-widen.3.6.s widen.3.7.s b.1.3 b.2.0 Z.0.1 Z.0.2 Z.0.3 b.2.1 b.2.2 x.0 r.0 b.2.3 a.0.0 zc.0.0 zc.0.1 a.0.1 zc.0.2 zc.0.3 turn_h.3 zm.0 A.0.0
-A.0.1 copy_h.3.0.s copy_h.3.1.s quant_h.3.0 quant_h.3.1 E.3.0 E.3.1 k.0.0 k.0.1 y.0.0 y.0.1 y.0.2 y.0.3 ma.1 q.0.0 q.0.1 E.3.2 mb.1 x.1 ma.2
-b.3.0 mb.2 b.3.1 E.3.3 b.3.2 r.1 x.2 K.0.0 w.0.0 K.0.1 w.0.1 K.0.2 w.0.2 K.0.3 w.0.3 b.3.3 a.1.0 a.1.1 A.1.0 A.1.1 Z.1.0 Z.1.1 ma.3 r.2
-k.1.0 Z.1.2 Z.1.3 k.1.1 mb.3 x.3 Z.2.0 Z.2.1 Z.2.2 Z.2.3 z.1.0 z.1.1 z.1.2 z.1.3 z.2.0 s.1 q.1.0 l1 q.1.1 r.3 z.2.1 y.1.0 y.1.1 K.1.0 y.1.2
-y.1.3 l2 z.2.2 z.2.3 l9 l3 K.1.1 l4 s.2 y.2.0 y.2.1 y.2.2 y.2.3 S.0.2 l5 a.2.0 l6 R.0.2 l7 a.2.1 K.1.2 K.1.3 l8 u.1.0 A.2.0 k.2.0 A.2.1
-k.2.1 u.1.1 a.3.0 a.3.1 u.1.2 Z.3.0 Z.3.1 Z.3.2 Z.3.3 l10.0.2 u.1.3 A.3.0 k.3.0 q.2.0 q.2.1 z.3.0 z.3.1 z.3.2 z.3.3 s.3 q.3.0 A.3.1 k.3.1
-K.2.0 T.0 gx.0.0.2 K.2.1 gx.0.2.4 y.3.0 y.3.1 y.3.2 y.3.3 S.2.4 q.3.1 R.2.4 K.2.2 K.2.3 v.1.0.2 l10.2.4 u.2.0 u.2.1 v.1.2.4 v.2.0.2 u.2.2
-u.2.3 v.2.2.4 K.3.0 u.3.0 K.3.1 K.3.2 K.3.3 u.3.1 u.3.2 v.3.0.2 v.3.2.3 u.3.3 v.3.3.4
+round_identity; spread_kb 0-1; widen_s 0 4-7; widen_v 0 0-3; turn_h 0; keep_kb 0-1; copy_h_v 0 0; copy_h_s 0 1;
+spread_kb 2-3; keep_kb 2-3; spread_g 0; quantize_h 0 0-1; widen_s 1 4-7; scores 0 0-1; widen_v 1 0-3; keep_g 0;
+spread_g 1; add_kb 0 0-1; turn_h 1; copy_h_s 1 0-1; quantize_h 1 0-1; scores 0 2-3; add_kb 0 2-3; widen_s 2 0-7;
+scores 1 0-3; keep_g 1; widen_s 3 0-7; add_kb 1 0; pair_max 0; turn_h 2; copy_h_s 2 0-1; turn_h 3; add_kb 1 1-3;
+copy_h_s 3 0-1; quantize_h 2 0-1; row_max 0; pair_max 1; spread_g 2-3; quantize_h 3 0-1; row_max 1; keep_g 2-3;
+scores 2 0-3; add_kb 2 0-2; exp_scores 0; exp_scores 1; invert_sum 0; add_kb 2 3; gain 0 0-1; scores 3 0-1;
+logits 0 0-3; add_kb 3 0-1; copy_logits 0 0-3; scores 3 2; copied_logit_max 0; turn_a 0 0-1; copy_a 0 0-1;
+quantize_a 0 0-1; scores 3 3; exp_logits 0 0-3; readout 0 0-3; pair_max 2; add_kb 3 2; row_max 2; invert_sum 1;
+add_kb 3 3; drain 0 0; gain 1 0-1; turn_a 1 0-1; pair_max 3; exp_scores 2; invert_sum 2; drain 0 1-3; copy_a 1 0;
+row_max 3; exp_scores 3; copy_a 1 1; logits 1 0-3; chunk_max 1 0-3; logits 2 0-3; quantize_a 1 0; gate_roots;
+logit_max 1; invert_sum 3; chunk_max 2 0-2; exp_logits 1 0-3; gate_square; quantize_a 1 1; chunk_max 2 3;
+gate_spread; gate_means; readout 1 0-2; gate_fourth; logit_max 2; gain 2 0; gate_odds; gain 2 1; turn_a 2 0-1;
+exp_logits 2 0-3; logits 3 0-3; gate_odds_1; gain 3 0; gate_lam; sum_logits 0 2; copy_a 2 0-1; gate_less_1;
+drain_gated 1 0-2; invert_logits 0 2; readout 1 3; quantize_a 2 0; chunk_max 3 0-1; gate_factor 0 2; chunk_max 3 2-3;
+quantize_a 2 1; logit_max 3; readout 2 0-1; gain 3 1; turn_a 3 0-1; readout 2 2-3; mix 1 0 2; gate_prob 0;
+mix_drained 0 0 2; mix_drained 0 2 4; exp_logits 3 0-3; sum_logits 2 4; copy_a 3 0-1; quantize_a 3 0;
+drain_gated 1 3; invert_logits 2 4; quantize_a 3 1; readout 3 0-3; gate_factor 2 4; mix 1 2 4; drain_gated 2 0-3;
+mix 2 0 2; drain_gated 3 0-3; mix 2 2 4; mix 3 0 2; mix 3 2 3; mix 3 3 4
 """
 
 
@@ -49,371 +58,404 @@ def tile_gatedmemoryattentionlmhead_kernel(
         psum = ctx.enter_context(tc.psum_pool(name="psum", bufs=8))
         ctx.enter_context(tc.manual_schedule())
 
-        def bank():
-            b = psum.tile([P, CHUNK], F32, name="bank")
-            return b
-
-        def quads(b):
-            return b[:].rearrange("p (q n) -> p q n", q=4)
-
-        hb = keep.tile([P, TILES, D], U8, name="hb", align_bytes=64)
-        hs = keep.tile([P, TILES * 8], F32, name="hs")
-        rows = keep.tile([P, CHUNK], BF16, name="rows")
-        rows_g = keep.tile([P, CHUNK], BF16, name="rows_g")
+        h_codes_in = keep.tile([P, TILES, D], U8, name="h_codes_in", align_bytes=64)
+        h_factors = keep.tile([P, TILES * BLOCKS], F32, name="h_factors")
+        kb_rows = keep.tile([P, CHUNK], BF16, name="kb_rows")
+        g_rows = keep.tile([P, CHUNK], BF16, name="g_rows")
         ident = keep.tile([P, P], F32, name="ident")
-        identb = keep.tile([P, P], BF16, name="identb")
-        root = keep.tile([P, 1], F32, name="root")
+        ident_bf = keep.tile([P, P], BF16, name="ident_bf")
         ones = keep.tile([P, P], F32, name="ones")
-        kplane = keep.tile([P, M], U8, name="kplane", align_bytes=64)
-        wplane = keep.tile([P, V], U8, name="wplane", align_bytes=64)
-        vplane = keep.tile([P, V], U8, name="vplane", align_bytes=64)
-        kw = [keep.tile([P, 2, CHUNK], U32, name=f"kw{c}", align_bytes=64) for c in range(NC)]
-        ww = [keep.tile([P, 2, CHUNK], U32, name=f"ww{c}", align_bytes=64) for c in range(NC)]
-        vw = [keep.tile([P, 4, CHUNK], U32, name=f"vw{c}", align_bytes=64) for c in range(NC)]
-        kbb = keep.tile([P, M], BF16, name="kbb")
-        g8p = keep.tile([P, 2, NC * 128, 2], BF16, name="g8p")
-        hq = [keep.tile([P, 2, P], U32, name=f"hq{i}", align_bytes=64) for i in range(TILES)]
-        hqs = [keep.tile([P, 2, P], U8, name=f"hqs{i}", align_bytes=64) for i in range(TILES)]
-        cmx = keep.tile([P, TILES], F32, name="cmx")
-        ncm = [cmx[:, i : i + 1] for i in range(TILES)]
+        root = keep.tile([P, 1], F32, name="root")
+        keys_planes = keep.tile([P, M], U8, name="keys_planes", align_bytes=64)
+        w_lm_planes = keep.tile([P, V], U8, name="w_lm_planes", align_bytes=64)
+        val_planes = keep.tile([P, V], U8, name="val_planes", align_bytes=64)
+        keys_w = [keep.tile([P, D_PASSES, CHUNK], U32, name=f"keys_w{c}", align_bytes=64) for c in range(CHUNKS)]
+        w_lm_w = [keep.tile([P, D_PASSES, CHUNK], U32, name=f"w_lm_w{c}", align_bytes=64) for c in range(CHUNKS)]
+        val_w = [keep.tile([P, M_PASSES, CHUNK], U32, name=f"val_w{c}", align_bytes=64) for c in range(CHUNKS)]
+        kb_all = keep.tile([P, M], BF16, name="kb_all")
+        g8_all = keep.tile([P, 2, M // 4, 2], BF16, name="g8_all")
+        h_q = [keep.tile([P, D_PASSES, P], U32, name=f"h_q{i}", align_bytes=64) for i in range(TILES)]
+        h_s = [keep.tile([P, D_PASSES, P], U8, name=f"h_s{i}", align_bytes=64) for i in range(TILES)]
+        neg_max = keep.tile([P, TILES], F32, name="neg_max")
         sums = keep.tile([P, TILES], F32, name="sums")
-        rs = keep.tile([P, TILES], F32, name="rs")
-        nz = keep.tile([P, TILES * NC], F32, name="nz")
-        nzm = keep.tile([P, TILES], F32, name="nzm")
-        zs = keep.tile([P, TILES * NC], F32, name="zs")
-        sz = keep.tile([P, TILES], F32, name="sz")
-        rsz = keep.tile([P, TILES], F32, name="rsz")
-        st = {k: keep.tile([P, w], F32, name=k) for k, w in (("p4", 1), ("junk4", 4), ("y", 1), ("gp", 1), ("ms", 1), ("r2", 4), ("r4", 4), ("qe", 4), ("q", 4), ("lam", 4), ("c0", 4), ("c1", 4))}
-        junk = keep.tile([P, P], F32, name="junk")
-        e_sb, e_b, ex, prob, a_bf, a_w, aq, aqs, o_sb = {}, {}, {}, {}, {}, {}, {}, {}, {}
-        eb, zb, kb_, ab = {}, {}, {}, {}
-        hw, hg, hbk, z_b = {}, {}, {}, {}
+        inv_sums = keep.tile([P, TILES], F32, name="inv_sums")
+        z_neg_max_chunk = keep.tile([P, TILES * CHUNKS], F32, name="z_neg_max_chunk")
+        z_neg_max = keep.tile([P, TILES], F32, name="z_neg_max")
+        z_sums_chunk = keep.tile([P, TILES * CHUNKS], F32, name="z_sums_chunk")
+        z_sums = keep.tile([P, TILES], F32, name="z_sums")
+        z_inv = keep.tile([P, TILES], F32, name="z_inv")
+        lam = keep.tile([P, TILES], F32, name="lam")
+        lam_less_1 = keep.tile([P, TILES], F32, name="lam_less_1")
+        p_factor = keep.tile([P, TILES], F32, name="p_factor")
+        sum_product = keep.tile([P, 1], F32, name="sum_product")
+        sum_root = keep.tile([P, 1], F32, name="sum_root")
+        mean_term = keep.tile([P, 1], F32, name="mean_term")
+        root_product = keep.tile([P, 1], F32, name="root_product")
+        inv_2 = keep.tile([P, TILES], F32, name="inv_2")
+        inv_4 = keep.tile([P, TILES], F32, name="inv_4")
+        odds_exp = keep.tile([P, TILES], F32, name="odds_exp")
+        odds = keep.tile([P, TILES], F32, name="odds")
+        few = keep.tile([P, TILES], F32, name="few")
+        many = keep.tile([P, P], F32, name="many")
 
-        h_rows = h_bytes.rearrange("(p i) k -> p i k", i=TILES)
-        out_rows = out.rearrange("(p i) n -> p i n", i=TILES)
+        h_bf, h_bank, h_pairs = {}, {}, {}
+        spread, score_bank, logit_bank, turn_bank, readout_bank = {}, {}, {}, {}, {}
+        scores_sb, half_max, w_exp, z_copy, prob, a_bf, a_pairs, a_q, a_s, mixed = {}, {}, {}, {}, {}, {}, {}, {}, {}, {}
 
-        def words(w):
-            return w.rearrange("g p n t -> p g (n t)").bitcast(I32)
+        def made(tiles, i, shape, dtype, name, bufs):
+            if i not in tiles:
+                tiles[i] = work.tile(shape, dtype, name=name, align_bytes=64, bufs=bufs)
+            return tiles[i]
 
-        def load_words(tiles, w, c):
-            nc.sync.dma_start(out=tiles[c][:].bitcast(I32), in_=words(w)[:, :, c * CHUNK : (c + 1) * CHUNK])
+        def new_bank():
+            return psum.tile([P, CHUNK], F32, name="bank")
 
-        def load_scales(plane, scales, groups, eng):
+        def col(t, i):
+            return t[:, i : i + 1]
+
+        def chunk(c):
+            return slice(c * CHUNK, (c + 1) * CHUNK)
+
+        def load_words(tiles, words, c):
+            view = words.rearrange("g p n t -> p g (n t)").bitcast(I32)
+            nc.sync.dma_start(out=tiles[c][:].bitcast(I32), in_=view[:, :, chunk(c)])
+
+        def load_scales(queue, planes, scales, passes):
             for q in range(4):
-                eng.dma_start(
-                    out=plane[32 * q : 32 * q + 4 * groups, :].bitcast(I32),
+                queue.dma_start(
+                    out=planes[32 * q : 32 * q + 4 * passes, :].bitcast(I32),
                     in_=scales.bitcast(I32)[:, 4 * q : 4 * q + 4, :],
                 )
 
-        nc.vector.memset(rows[:], 0.0)
-        nc.vector.memset(kplane[:].bitcast(I32), 0)
+        h_rows = h_bytes.rearrange("(p i) k -> p i k", i=TILES)
+        out_rows = out.rearrange("(p i) n -> p i n", i=TILES)
+        as_rows = "(c n) -> c n"
+
+        nc.vector.memset(keys_planes[:].bitcast(I32), 0)
+        nc.vector.memset(kb_rows[:], 0.0)
         nc.vector.memset(ones[:], 0.0)
-        nc.vector.memset(rows_g[:], 0.0)
-        nc.vector.memset(wplane[:].bitcast(I32), 0)
-        nc.vector.memset(vplane[:].bitcast(I32), 0)
-        nc.sync.dma_start(out=hb[:, 0, :], in_=h_rows[:, 0, :])
-        nc.scalar.dma_start(out=hs[:], in_=h_scale.rearrange("(p i) j -> p (i j)", i=TILES))
-        nc.sync.dma_start(out=rows[0:4, :], in_=kb.rearrange("(c n) -> c n", c=NC))
-        load_words(kw, keys_words, 0)
-        load_scales(kplane, keys_scales, 2, nc.scalar)
-        nc.sync.dma_start(out=hb[:, 1:TILES, :], in_=h_rows[:, 1:TILES, :])
+        nc.vector.memset(g_rows[:], 0.0)
+        nc.vector.memset(w_lm_planes[:].bitcast(I32), 0)
+        nc.vector.memset(val_planes[:].bitcast(I32), 0)
+        nc.sync.dma_start(out=h_codes_in[:, 0, :], in_=h_rows[:, 0, :])
+        nc.scalar.dma_start(out=h_factors[:], in_=h_scale.rearrange("(p i) b -> p (i b)", i=TILES))
+        nc.scalar.dma_start(out=kb_rows[0:CHUNKS, :], in_=kb.rearrange(as_rows, c=CHUNKS))
+        load_scales(nc.sync, keys_planes, keys_scales, D_PASSES)
+        load_words(keys_w, keys_words, 0)
+        load_words(keys_w, keys_words, 1)
+        nc.sync.dma_start(out=h_codes_in[:, 1:TILES, :], in_=h_rows[:, 1:TILES, :])
+        nc.scalar.dma_start(out=g_rows[0:CHUNKS, :], in_=g.rearrange(as_rows, c=CHUNKS))
         nc.scalar.activation(out=ones[:], in_=ones[:], func=ACT.Exp)
         make_identity(nc, ident[:])
-        nc.gpsimd.dma_start(out=rows_g[0:4, :], in_=g.rearrange("(c n) -> c n", c=NC))
-        nc.gpsimd.memset(root[:], 1.0 / 128.0)
-        for c in range(1, NC):
-            load_words(kw, keys_words, c)
-        load_scales(wplane, w_lm_scales, 2, nc.gpsimd)
-        load_scales(vplane, val_scales, 4, nc.gpsimd)
-        for c in range(NC):
-            load_words(ww, w_lm_words, c)
-        for c in range(NC):
-            load_words(vw, val_words, c)
+        nc.gpsimd.memset(root[:], 1.0 / P)
+        for c in range(2, CHUNKS):
+            load_words(keys_w, keys_words, c)
+        load_scales(nc.sync, w_lm_planes, w_lm_scales, D_PASSES)
+        load_scales(nc.gpsimd, val_planes, val_scales, M_PASSES)
+        for c in range(CHUNKS):
+            load_words(w_lm_w, w_lm_words, c)
+        for c in range(CHUNKS):
+            load_words(val_w, val_words, c)
 
-        def identb_():
-            nc.vector.tensor_copy(out=identb[:], in_=ident[:])
+        def spread_row(rows, key, c):
+            spread[key, c] = new_bank()
+            nc.tensor.matmul(
+                spread[key, c][:], lhsT=col(ident_bf, c).to_broadcast([P, P]), rhs=rows[:], start=True, stop=True
+            )
 
-        def spread(c):
-            b = bank()
-            ab[("row", c)] = b
-            r = rows if c < NC else rows_g
-            nc.tensor.matmul(b[:], lhsT=identb[:, c % NC : c % NC + 1].to_broadcast([P, P]), rhs=r[:], start=True, stop=True)
+        def round_identity():
+            nc.vector.tensor_copy(out=ident_bf[:], in_=ident[:])
+
+        def spread_kb(c):
+            spread_row(kb_rows, "kb", c)
+
+        def spread_g(c):
+            spread_row(g_rows, "g", c)
 
         def keep_kb(c):
-            nc.scalar.copy(out=kbb[:, c * CHUNK : (c + 1) * CHUNK], in_=ab[("row", c)][:])
+            nc.scalar.copy(out=kb_all[:, chunk(c)], in_=spread["kb", c][:])
 
         def keep_g(c):
             nc.scalar.activation(
-                out=g8p[:, :, c * P : (c + 1) * P, :],
-                in_=ab["row", NC + c][:].rearrange("p (w u e) -> p u w e", u=2, e=2),
+                out=g8_all[:, :, c * P : (c + 1) * P, :],
+                in_=spread["g", c][:].rearrange("p (w u e) -> p u w e", u=2, e=2),
                 func=ACT.Copy,
                 scale=8.0,
             )
 
-        def widen(i, b, eng):
-            if i not in hw:
-                hw[i] = work.tile([P, D], BF16, name="hw", align_bytes=64, bufs=2)
-            o, x, s = hw[i][:, P * b : P * b + P], hb[:, i, P * b : P * b + P].bitcast(FP8), hs[:, 8 * i + b : 8 * i + b + 1]
-            if eng == "v":
-                nc.vector.tensor_scalar(out=o, in0=x, scalar1=s, scalar2=None, op0=ALU.mult)
-            else:
-                nc.scalar.activation(out=o, in_=x, func=ACT.Copy, scale=s)
+        def widen(i, b):
+            cols = slice(b * BLOCK, (b + 1) * BLOCK)
+            h = made(h_bf, i, [P, D], BF16, "h_bf", 2)
+            return h[:, cols], h_codes_in[:, i, cols].bitcast(FP8), col(h_factors, BLOCKS * i + b)
+
+        def widen_v(i, b):
+            to, codes, factor = widen(i, b)
+            nc.vector.tensor_scalar(out=to, in0=codes, scalar1=factor, scalar2=None, op0=ALU.mult)
+
+        def widen_s(i, b):
+            to, codes, factor = widen(i, b)
+            nc.scalar.activation(out=to, in_=codes, func=ACT.Copy, scale=factor)
 
         def turn_h(i):
-            hbk[i] = bank()
-            w = hw[i][:].bitcast(F32)
-            for gu in range(4):
-                gg, u = gu // 2, gu % 2
-                nc.tensor.transpose(quads(hbk[i])[:, gu, :], w[:, 256 * gg + u : 256 * (gg + 1) : 2], ident[:])
+            h_bank[i] = new_bank()
+            turned = h_bank[i][:].rearrange("p (gu n) -> p gu n", n=P)
+            words = h_bf[i][:].bitcast(F32)
+            for gu in range(2 * D_PASSES):
+                first = PAIR * (gu // 2)
+                nc.tensor.transpose(turned[:, gu, :], words[:, first + gu % 2 : first + PAIR : 2], ident[:])
 
-        def copy_h(i, gg, eng):
-            if i not in hg:
-                hg[i] = work.tile([P, 2, 4 * P], BF16, name="hg", align_bytes=64, bufs=2)
-            o = hg[i][:, gg, :].bitcast(F32).rearrange("p (n u) -> p n u", u=2)
-            x = quads(hbk[i])[:, 2 * gg : 2 * gg + 2, :].rearrange("p u n -> p n u")
-            if eng == "v":
-                nc.vector.tensor_copy(out=o, in_=x)
-            else:
-                nc.scalar.copy(out=o, in_=x)
+        def h_copy(i, q):
+            pairs = made(h_pairs, i, [P, D_PASSES, 4 * P], BF16, "h_pairs", 2)
+            to = pairs[:, q, :].bitcast(F32).rearrange("p (n u) -> p n u", u=2)
+            return to, h_bank[i][:].rearrange("p (q u n) -> p q n u", u=2, n=P)[:, q, :, :]
 
-        def quant_h(i, gg):
-            nc.vector.quantize_mx(out=hq[i][:, gg, :].bitcast(FP8X4), scales=hqs[i][:, gg, :], in_=hg[i][:, gg, :])
+        def copy_h_v(i, q):
+            to, turned = h_copy(i, q)
+            nc.vector.tensor_copy(out=to, in_=turned)
 
-        def product(b, i, codes, scales, groups, w, plane, c):
-            for gg in range(groups):
+        def copy_h_s(i, q):
+            to, turned = h_copy(i, q)
+            nc.scalar.copy(out=to, in_=turned)
+
+        def quantize_h(i, q):
+            nc.vector.quantize_mx(out=h_q[i][:, q, :].bitcast(FP8X4), scales=h_s[i][:, q, :], in_=h_pairs[i][:, q, :])
+
+        def product(bank, codes, scales, words, planes, passes, c):
+            for q in range(passes):
                 nc.tensor.matmul_mx(
-                    out=b[:],
-                    lhsT=codes[i][:, gg, :].bitcast(FP8X4),
-                    lhsT_scale=scales[i][:, gg, :],
-                    rhs=w[c][:, gg, :].bitcast(FP8X4),
-                    rhs_scale=plane[4 * gg : P, c * CHUNK : (c + 1) * CHUNK],
-                    start=(gg == 0),
-                    stop=(gg == groups - 1),
+                    out=bank[:],
+                    lhsT=codes[:, q, :].bitcast(FP8X4),
+                    lhsT_scale=scales[:, q, :],
+                    rhs=words[c][:, q, :].bitcast(FP8X4),
+                    rhs_scale=planes[4 * q : P, chunk(c)],
+                    start=(q == 0),
+                    stop=(q == passes - 1),
                 )
 
-        def E(i, c):
-            eb[i, c] = bank()
-            product(eb[i, c], i, hq, hqs, 2, kw, kplane, c)
+        def scores(i, c):
+            score_bank[i, c] = new_bank()
+            product(score_bank[i, c], h_q[i], h_s[i], keys_w, keys_planes, D_PASSES, c)
 
-        def b(i, c):
-            if i not in e_sb:
-                e_sb[i] = work.tile([P, NC, CHUNK], F32, name="e_sb", bufs=3)
+        def logits(i, c):
+            logit_bank[i, c] = new_bank()
+            product(logit_bank[i, c], h_q[i], h_s[i], w_lm_w, w_lm_planes, D_PASSES, c)
+
+        def readout(i, c):
+            readout_bank[i, c] = new_bank()
+            product(readout_bank[i, c], a_q[i], a_s[i], val_w, val_planes, M_PASSES, c)
+
+        def add_kb(i, c):
+            e = made(scores_sb, i, [P, CHUNKS, CHUNK], F32, "scores_sb", 3)
             nc.vector.scalar_tensor_tensor(
-                out=e_sb[i][:, c, :], in0=eb[i, c][:], scalar=1.0 / 20.0, in1=kbb[:, c * CHUNK : (c + 1) * CHUNK], op0=ALU.mult, op1=ALU.add
+                out=e[:, c, :], in0=score_bank[i, c][:], scalar=1.0 / 20.0, in1=kb_all[:, chunk(c)], op0=ALU.mult, op1=ALU.add
             )
 
-        def c(i):
-            e_b[i] = work.tile([P, M], BF16, name="e_b", bufs=2)
-            nc.gpsimd.tensor_scalar(
-                out=e_b[i][:], in0=e_sb[i][:].rearrange("p c n -> p (c n)"), scalar1=1.0, scalar2=0.0, op0=ALU.mult, op1=ALU.add
-            )
-
-        def cs(i):
-            e_b[i] = work.tile([P, M], BF16, name="e_b", bufs=2)
-            nc.scalar.copy(out=e_b[i][:], in_=e_sb[i][:].rearrange("p c n -> p (c n)"))
-
-        def m(i):
-            nc.vector.tensor_scalar(
-                out=e_b[i][:], in0=e_b[i][:], scalar1=-1.0, scalar2=None, op0=ALU.mult, op1=ALU.min, accum_out=ncm[i]
-            )
-
-        def ma(i):
-            e_b[i] = work.tile([P, M], BF16, name="e_b", bufs=2)
+        def pair_max(i):
+            t = made(half_max, i, [P, M // 2], BF16, "half_max", 2)
             nc.vector.tensor_tensor(
-                out=e_b[i][:, 0 : M // 2].rearrange("p (c n) -> p c n", c=2), in0=e_sb[i][:, 0:2, :], in1=e_sb[i][:, 2:4, :], op=ALU.max
+                out=t[:].rearrange("p (c n) -> p c n", c=2), in0=scores_sb[i][:, 0:2, :], in1=scores_sb[i][:, 2:4, :], op=ALU.max
             )
 
-        def mb(i):
-            h = e_b[i][:, 0 : M // 2]
-            nc.vector.tensor_scalar(out=h, in0=h, scalar1=-1.0, scalar2=None, op0=ALU.mult, op1=ALU.min, accum_out=ncm[i])
+        def row_max(i):
+            t = half_max[i][:]
+            nc.vector.tensor_scalar(
+                out=t, in0=t, scalar1=-1.0, scalar2=None, op0=ALU.mult, op1=ALU.min, accum_out=col(neg_max, i)
+            )
 
-        def mf(i):
-            nc.vector.tensor_reduce(out=ncm[i], in_=e_sb[i][:].rearrange("p c n -> p (c n)"), axis=AX.X, op=ALU.max, negate=True)
-
-        def x(i):
-            ex[i] = work.tile([P, 2, NC * 128, 2], F32, name="ex", bufs=3)
+        def exp_scores(i):
+            w_exp[i] = work.tile([P, 2, M // 4, 2], F32, name="w_exp", bufs=3)
             nc.scalar.activation(
-                out=ex[i][:],
-                in_=e_sb[i][:].rearrange("p c (w u e) -> p u (c w) e", u=2, e=2),
+                out=w_exp[i][:],
+                in_=scores_sb[i][:].rearrange("p c (w u e) -> p u (c w) e", u=2, e=2),
                 func=ACT.Exp,
-                bias=ncm[i],
-                accum_out=sums[:, i : i + 1],
+                bias=col(neg_max, i),
+                accum_out=col(sums, i),
             )
 
-        def r(i):
-            nc.vector.reciprocal(out=rs[:, i : i + 1], in_=sums[:, i : i + 1])
+        def invert_sum(i):
+            nc.vector.reciprocal(out=col(inv_sums, i), in_=col(sums, i))
 
-        def a(i, f):
-            if i not in a_bf:
-                a_bf[i] = work.tile([P, 2, NC * 256], BF16, name="a_bf", align_bytes=64, bufs=2)
-            s = slice(f * 512, f * 512 + 512)
+        def gain(i, half):
+            a = made(a_bf, i, [P, 2, M // 2], BF16, "a_bf", 2)
+            cols = slice(half * (M // 4), (half + 1) * (M // 4))
             nc.vector.scalar_tensor_tensor(
-                out=a_bf[i][:, :, s],
-                in0=ex[i][:].rearrange("p u w e -> p u (w e)")[:, :, s],
-                scalar=rs[:, i : i + 1],
-                in1=g8p[:].rearrange("p u w e -> p u (w e)")[:, :, s],
+                out=a[:, :, cols],
+                in0=w_exp[i][:].rearrange("p u w e -> p u (w e)")[:, :, cols],
+                scalar=col(inv_sums, i),
+                in1=g8_all[:].rearrange("p u w e -> p u (w e)")[:, :, cols],
                 op0=ALU.mult,
                 op1=ALU.mult,
             )
 
-        def zc(i, c):
-            if i not in z_b:
-                z_b[i] = work.tile([P, NC, CHUNK], BF16, name="z_b", bufs=1)
-            nc.scalar.copy(out=z_b[i][:, c, :], in_=zb[i, c][:])
+        def turn_a(i, half):
+            turn_bank[i, half] = new_bank()
+            turned = turn_bank[i, half][:].rearrange("p (q u n) -> p q u n", u=2, n=P)
+            words = a_bf[i][:].bitcast(F32)
+            for q in range(2):
+                for u in range(2):
+                    first = (2 * half + q) * P
+                    nc.tensor.transpose(turned[:, q, u, :], words[:, u, first : first + P], ident[:])
 
-        def zm(i):
-            zz = z_b[i][:].rearrange("p c n -> p (c n)")
-            nc.vector.tensor_scalar(out=zz, in0=zz, scalar1=-1.0, scalar2=None, op0=ALU.mult, op1=ALU.min, accum_out=nzm[:, i : i + 1])
+        def copy_a(i, half):
+            pairs = made(a_pairs, i, [P, M_PASSES, 4 * P], BF16, "a_pairs", 2)
+            nc.scalar.copy(
+                out=pairs[:, 2 * half : 2 * half + 2, :].bitcast(F32).rearrange("p q (n u) -> p q n u", u=2),
+                in_=turn_bank[i, half][:].rearrange("p (q u n) -> p q n u", u=2, n=P),
+            )
 
-        def A(i, f):
-            ab[i, f] = bank()
-            w = a_bf[i][:].rearrange("p u w -> p (u w)").bitcast(F32)
-            for ju in range(4):
-                j, u = 2 * f + ju // 2, ju % 2
-                nc.tensor.transpose(quads(ab[i, f])[:, ju, :], w[:, 512 * u + 128 * j : 512 * u + 128 * j + 128], ident[:])
-
-        def k(i, f, eng="s"):
-            if i not in a_w:
-                a_w[i] = work.tile([P, 4, 4 * P], BF16, name="a_w", align_bytes=64, bufs=2)
-            o = a_w[i][:, 2 * f : 2 * f + 2, :].rearrange("p j k -> p (j k)").bitcast(F32).rearrange("p (j n u) -> p j n u", j=2, u=2)
-            xx = ab[i, f][:].rearrange("p (j u n) -> p j n u", j=2, u=2)
-            if eng == "s":
-                nc.scalar.copy(out=o, in_=xx)
-            else:
-                nc.vector.tensor_copy(out=o, in_=xx)
-
-        def q(i, f):
-            if i not in aq:
-                aq[i] = work.tile([P, 4, P], U32, name="aq", align_bytes=64, bufs=4)
-                aqs[i] = work.tile([P, 4, P], U8, name="aqs", align_bytes=64, bufs=4)
+        def quantize_a(i, half):
+            two = slice(2 * half, 2 * half + 2)
+            codes = made(a_q, i, [P, M_PASSES, P], U32, "a_q", 4)
+            scales = made(a_s, i, [P, M_PASSES, P], U8, "a_s", 4)
             nc.vector.quantize_mx(
-                out=aq[i][:, 2 * f : 2 * f + 2, :].rearrange("p j n -> p (j n)").bitcast(FP8X4),
-                scales=aqs[i][:, 2 * f : 2 * f + 2, :].rearrange("p j n -> p (j n)"),
-                in_=a_w[i][:, 2 * f : 2 * f + 2, :].rearrange("p j k -> p (j k)"),
+                out=codes[:, two, :].rearrange("p q n -> p (q n)").bitcast(FP8X4),
+                scales=scales[:, two, :].rearrange("p q n -> p (q n)"),
+                in_=a_pairs[i][:, two, :].rearrange("p q k -> p (q k)"),
             )
 
-        def Z(i, c):
-            zb[i, c] = bank()
-            product(zb[i, c], i, hq, hqs, 2, ww, wplane, c)
-
-        def z(i, c):
-            nc.vector.tensor_reduce(out=nz[:, NC * i + c : NC * i + c + 1], in_=zb[i, c][:], axis=AX.X, op=ALU.max, negate=True)
-
-        def s(i):
-            nc.vector.tensor_reduce(out=nzm[:, i : i + 1], in_=nz[:, NC * i : NC * i + NC], axis=AX.X, op=ALU.min)
-
-        def y(i, c):
-            if i not in prob:
-                prob[i] = work.tile([P, NC, CHUNK], F32, name="prob", bufs=4)
-            nc.scalar.activation(
-                out=prob[i][:, c, :], in_=zb[i, c][:], func=ACT.Exp, bias=nzm[:, i : i + 1], accum_out=zs[:, NC * i + c : NC * i + c + 1]
-            )
-
-        def l1():
-            nc.vector.tensor_scalar(out=st["junk4"][:], in0=sums[:], scalar1=1.0, scalar2=None, op0=ALU.mult, op1=ALU.mult, accum_out=st["p4"][:])
-            nc.gpsimd.tensor_tensor(out=st["y"][:], in0=st["p4"][:], in1=root[:], op=ALU.pow)
-
-        def l2():
-            nc.vector.tensor_tensor(out=st["r2"][:], in0=rs[:], in1=rs[:], op=ALU.mult)
-
-        def l9():
-            nc.vector.tensor_tensor(out=st["r4"][:], in0=st["r2"][:], in1=st["r2"][:], op=ALU.mult)
-
-        def l3():
-            ab["gate"] = bank()
-            nc.tensor.matmul(ab["gate"][:, P : P + TILES], lhsT=ones[:], rhs=cmx[:], start=True, stop=True)
-            nc.tensor.transpose(ab["gate"][:, 0:P], st["y"][:].to_broadcast([P, P]), ident[:])
-
-        def l4():
-            nc.vector.tensor_scalar(
-                out=st["junk4"][:], in0=ab["gate"][:, P : P + TILES], scalar1=-4.0 / N, scalar2=None, op0=ALU.mult, op1=ALU.add, accum_out=st["ms"][:]
-            )
-            nc.vector.tensor_scalar(out=junk[:], in0=ab["gate"][:, 0:P], scalar1=1.0, scalar2=None, op0=ALU.mult, op1=ALU.mult, accum_out=st["gp"][:])
-            nc.scalar.activation(out=st["qe"][:], in_=cmx[:], func=ACT.Exp, scale=4.0, bias=st["ms"][:])
-
-        def l5():
-            nc.vector.tensor_tensor(out=st["q"][:], in0=st["qe"][:], in1=st["r4"][:], op=ALU.mult)
-
-        def l6():
-            nc.vector.tensor_scalar(out=st["q"][:], in0=st["q"][:], scalar1=st["gp"][:], scalar2=1.0, op0=ALU.mult, op1=ALU.add)
-
-        def l7():
-            nc.vector.reciprocal(out=st["lam"][:], in_=st["q"][:])
-
-        def l8():
-            nc.vector.tensor_scalar(out=st["c0"][:], in0=st["lam"][:], scalar1=-1.0, scalar2=None, op0=ALU.add)
-
-        def S(lo, hi):
+        def chunk_max(i, c):
             nc.vector.tensor_reduce(
-                out=sz[:, lo:hi], in_=zs[:, NC * lo : NC * hi].rearrange("p (i c) -> p i c", c=NC), axis=AX.X, op=ALU.add
+                out=col(z_neg_max_chunk, CHUNKS * i + c), in_=logit_bank[i, c][:], axis=AX.X, op=ALU.max, negate=True
             )
 
-        def R(lo, hi):
-            nc.vector.reciprocal(out=rsz[:, lo:hi], in_=sz[:, lo:hi])
+        def logit_max(i):
+            chunks = z_neg_max_chunk[:, CHUNKS * i : CHUNKS * (i + 1)]
+            nc.vector.tensor_reduce(out=col(z_neg_max, i), in_=chunks, axis=AX.X, op=ALU.min)
 
-        def l10(lo, hi):
-            nc.vector.scalar_tensor_tensor(
-                out=st["c1"][:, lo:hi], in0=st["c0"][:, lo:hi], scalar=-float(V), in1=rsz[:, lo:hi], op0=ALU.mult, op1=ALU.mult
+        def copy_logits(i, c):
+            z = made(z_copy, i, [P, CHUNKS, CHUNK], BF16, "z_copy", 1)
+            nc.scalar.copy(out=z[:, c, :], in_=logit_bank[i, c][:])
+
+        def copied_logit_max(i):
+            z = z_copy[i][:].rearrange("p c n -> p (c n)")
+            nc.vector.tensor_scalar(
+                out=z, in0=z, scalar1=-1.0, scalar2=None, op0=ALU.mult, op1=ALU.min, accum_out=col(z_neg_max, i)
             )
 
-        def K(i, c):
-            kb_[i, c] = bank()
-            product(kb_[i, c], i, aq, aqs, 4, vw, vplane, c)
-
-        def T(i, lo=0, hi=NC, eng="g"):
-            t = prob[i][:, lo:hi, :].rearrange("p c n -> p (c n)")
-            if eng == "g":
-                nc.gpsimd.tensor_scalar(out=t, in0=t, scalar1=st["c1"][:, i : i + 1], scalar2=st["c0"][:, i : i + 1], op0=ALU.mult, op1=ALU.add)
-            else:
-                nc.scalar.activation(out=t, in_=t, func=ACT.Identity, scale=st["c1"][:, i : i + 1], bias=st["c0"][:, i : i + 1])
-
-        def f(i, c):
-            if i not in o_sb:
-                o_sb[i] = work.tile([P, NC, CHUNK], F32, name="o_sb", bufs=2)
-            nc.vector.scalar_tensor_tensor(
-                out=o_sb[i][:, c, :], in0=kb_[i, c][:], scalar=st["lam"][:, i : i + 1], in1=prob[i][:, c, :], op0=ALU.mult, op1=ALU.add
-            )
-            nc.sync.dma_start(out=out_rows[:, i, c * CHUNK : (c + 1) * CHUNK], in_=o_sb[i][:, c, :])
-
-        def u(i, c):
-            if i not in o_sb:
-                o_sb[i] = work.tile([P, NC, CHUNK], F32, name="o_sb", bufs=2)
+        def exp_logits(i, c):
+            e = made(prob, i, [P, CHUNKS, CHUNK], F32, "prob", 4)
             nc.scalar.activation(
-                out=o_sb[i][:, c, :], in_=kb_[i, c][:], func=ACT.Identity, scale=st["lam"][:, i : i + 1], bias=st["c0"][:, i : i + 1]
+                out=e[:, c, :],
+                in_=logit_bank[i, c][:],
+                func=ACT.Exp,
+                bias=col(z_neg_max, i),
+                accum_out=col(z_sums_chunk, CHUNKS * i + c),
             )
 
-        def w(i, c):
-            if i not in o_sb:
-                o_sb[i] = work.tile([P, NC, CHUNK], F32, name="o_sb", bufs=2)
-            nc.scalar.copy(out=o_sb[i][:, c, :], in_=kb_[i, c][:])
+        def sum_logits(lo, hi):
+            chunks = z_sums_chunk[:, CHUNKS * lo : CHUNKS * hi].rearrange("p (i c) -> p i c", c=CHUNKS)
+            nc.vector.tensor_reduce(out=z_sums[:, lo:hi], in_=chunks, axis=AX.X, op=ALU.add)
 
-        def gx(i, lo, hi):
-            nc.vector.scalar_tensor_tensor(
-                out=o_sb[i][:, lo:hi, :].rearrange("p c n -> p (c n)"),
-                in0=o_sb[i][:, lo:hi, :].rearrange("p c n -> p (c n)"),
-                scalar=st["lam"][:, i : i + 1],
-                in1=prob[i][:, lo:hi, :].rearrange("p c n -> p (c n)"),
+        def invert_logits(lo, hi):
+            nc.vector.reciprocal(out=z_inv[:, lo:hi], in_=z_sums[:, lo:hi])
+
+        def gate_roots():
+            nc.vector.tensor_scalar(
+                out=few[:], in0=sums[:], scalar1=1.0, scalar2=None, op0=ALU.mult, op1=ALU.mult, accum_out=sum_product[:]
+            )
+            nc.gpsimd.tensor_tensor(out=sum_root[:], in0=sum_product[:], in1=root[:], op=ALU.pow)
+
+        def gate_square():
+            nc.vector.tensor_tensor(out=inv_2[:], in0=inv_sums[:], in1=inv_sums[:], op=ALU.mult)
+
+        def gate_fourth():
+            nc.vector.tensor_tensor(out=inv_4[:], in0=inv_2[:], in1=inv_2[:], op=ALU.mult)
+
+        def gate_spread():
+            spread["gate"] = new_bank()
+            nc.tensor.matmul(spread["gate"][:, P : P + TILES], lhsT=ones[:], rhs=neg_max[:], start=True, stop=True)
+            nc.tensor.transpose(spread["gate"][:, 0:P], sum_root[:].to_broadcast([P, P]), ident[:])
+
+        def gate_means():
+            bank = spread["gate"]
+            nc.vector.tensor_scalar(
+                out=few[:],
+                in0=bank[:, P : P + TILES],
+                scalar1=-4.0 / N,
+                scalar2=None,
                 op0=ALU.mult,
                 op1=ALU.add,
+                accum_out=mean_term[:],
             )
-            nc.sync.dma_start(out=out_rows[:, i, lo * CHUNK : hi * CHUNK], in_=o_sb[i][:, lo:hi, :].rearrange("p c n -> p (c n)"))
+            nc.vector.tensor_scalar(
+                out=many[:], in0=bank[:, 0:P], scalar1=1.0, scalar2=None, op0=ALU.mult, op1=ALU.mult, accum_out=root_product[:]
+            )
+            nc.scalar.activation(out=odds_exp[:], in_=neg_max[:], func=ACT.Exp, scale=4.0, bias=mean_term[:])
 
-        def v(i, lo, hi):
-            nc.vector.scalar_tensor_tensor(
-                out=o_sb[i][:, lo:hi, :].rearrange("p c n -> p (c n)"),
-                in0=prob[i][:, lo:hi, :].rearrange("p c n -> p (c n)"),
-                scalar=st["c1"][:, i : i + 1],
-                in1=o_sb[i][:, lo:hi, :].rearrange("p c n -> p (c n)"),
-                op0=ALU.mult,
-                op1=ALU.add,
+        def gate_odds():
+            nc.vector.tensor_tensor(out=odds[:], in0=odds_exp[:], in1=inv_4[:], op=ALU.mult)
+
+        def gate_odds_1():
+            nc.vector.tensor_scalar(
+                out=odds[:], in0=odds[:], scalar1=root_product[:], scalar2=1.0, op0=ALU.mult, op1=ALU.add
             )
-            nc.sync.dma_start(out=out_rows[:, i, lo * CHUNK : hi * CHUNK], in_=o_sb[i][:, lo:hi, :].rearrange("p c n -> p (c n)"))
+
+        def gate_lam():
+            nc.vector.reciprocal(out=lam[:], in_=odds[:])
+
+        def gate_less_1():
+            nc.vector.tensor_scalar(out=lam_less_1[:], in0=lam[:], scalar1=-1.0, scalar2=None, op0=ALU.add)
+
+        def gate_factor(lo, hi):
+            nc.vector.scalar_tensor_tensor(
+                out=p_factor[:, lo:hi], in0=lam_less_1[:, lo:hi], scalar=-float(V), in1=z_inv[:, lo:hi], op0=ALU.mult, op1=ALU.mult
+            )
+
+        def flat(t, lo, hi):
+            return t[:, lo:hi, :].rearrange("p c n -> p (c n)")
+
+        def store(i, lo, hi):
+            nc.sync.dma_start(out=out_rows[:, i, lo * CHUNK : hi * CHUNK], in_=flat(mixed[i], lo, hi))
+
+        def drain(i, c):
+            o = made(mixed, i, [P, CHUNKS, CHUNK], F32, "mixed", 2)
+            nc.scalar.copy(out=o[:, c, :], in_=readout_bank[i, c][:])
+
+        def gate_prob(i):
+            p = flat(prob[i], 0, CHUNKS)
+            nc.scalar.activation(out=p, in_=p, func=ACT.Identity, scale=col(p_factor, i), bias=col(lam_less_1, i))
+
+        def mix_drained(i, lo, hi):
+            o = flat(mixed[i], lo, hi)
+            nc.vector.scalar_tensor_tensor(
+                out=o, in0=o, scalar=col(lam, i), in1=flat(prob[i], lo, hi), op0=ALU.mult, op1=ALU.add
+            )
+            store(i, lo, hi)
+
+        def drain_gated(i, c):
+            o = made(mixed, i, [P, CHUNKS, CHUNK], F32, "mixed", 2)
+            nc.scalar.activation(
+                out=o[:, c, :], in_=readout_bank[i, c][:], func=ACT.Identity, scale=col(lam, i), bias=col(lam_less_1, i)
+            )
+
+        def mix(i, lo, hi):
+            o = flat(mixed[i], lo, hi)
+            nc.vector.scalar_tensor_tensor(
+                out=o, in0=flat(prob[i], lo, hi), scalar=col(p_factor, i), in1=o, op0=ALU.mult, op1=ALU.add
+            )
+            store(i, lo, hi)
 
         steps = {
-            "keep_g": keep_g, "identb": identb_, "spread": spread, "keep_kb": keep_kb, "widen": widen, "turn_h": turn_h, "copy_h": copy_h, "quant_h": quant_h,
-            "E": E, "b": b, "c": c, "u": u, "v": v, "w": w, "gx": gx, "cs": cs, "m": m, "mf": mf, "ma": ma, "mb": mb, "x": x, "r": r, "a": a, "A": A, "k": k, "q": q, "Z": Z, "z": z, "s": s, "y": y, "S": S,
-            "zc": zc, "zm": zm, "l1": l1, "l2": l2, "l3": l3, "l4": l4, "l5": l5, "l6": l6, "l7": l7, "l8": l8, "l9": l9, "l10": l10, "R": R, "K": K, "T": T, "f": f,
+            "widen_v": widen_v, "widen_s": widen_s, "round_identity": round_identity, "spread_kb": spread_kb,
+            "spread_g": spread_g, "keep_kb": keep_kb, "keep_g": keep_g, "turn_h": turn_h, "copy_h_v": copy_h_v,
+            "copy_h_s": copy_h_s, "quantize_h": quantize_h, "scores": scores, "logits": logits, "readout": readout,
+            "add_kb": add_kb, "pair_max": pair_max, "row_max": row_max, "exp_scores": exp_scores,
+            "invert_sum": invert_sum, "gain": gain, "turn_a": turn_a, "copy_a": copy_a, "quantize_a": quantize_a,
+            "chunk_max": chunk_max, "logit_max": logit_max, "copy_logits": copy_logits,
+            "copied_logit_max": copied_logit_max, "exp_logits": exp_logits, "sum_logits": sum_logits,
+            "invert_logits": invert_logits, "gate_roots": gate_roots, "gate_square": gate_square,
+            "gate_fourth": gate_fourth, "gate_spread": gate_spread, "gate_means": gate_means, "gate_odds": gate_odds,
+            "gate_odds_1": gate_odds_1, "gate_lam": gate_lam, "gate_less_1": gate_less_1, "gate_factor": gate_factor,
+            "drain": drain, "gate_prob": gate_prob, "mix_drained": mix_drained, "drain_gated": drain_gated,
+            "mix": mix,
         }
-        for token in ORDER.split():
-            parts = token.split(".")
-            steps[parts[0]](*[int(v) if v not in ("v", "s", "g") else v for v in parts[1:]])
+        for entry in ORDER.replace("\n", " ").split(";"):
+            words = entry.split()
+            step, fixed, last = steps[words[0]], [int(w) for w in words[1:-1]], words[-1].split("-")
+            if len(words) == 1:
+                step()
+            elif len(last) == 1:
+                step(*fixed, int(last[0]))
+            else:
+                for index in range(int(last[0]), int(last[1]) + 1):
+                    step(*fixed, index)

from contextlib import ExitStack

import concourse.mybir as mybir
from concourse.masks import make_identity

F32 = mybir.dt.float32
BF16 = mybir.dt.bfloat16
U32 = mybir.dt.uint32
I32 = mybir.dt.int32
U8 = mybir.dt.uint8
FP8 = mybir.dt.float8_e4m3fn
FP8X4 = mybir.dt.float8_e4m3fn_x4
ALU = mybir.AluOpType
ACT = mybir.ActivationFunctionType
AX = mybir.AxisListType

P = 128
N, D, M, V = 512, 1024, 2048, 2048
TILES = N // P
CHUNK = 512
CHUNKS = V // CHUNK
BLOCK = 128
BLOCKS = D // BLOCK
D_PASSES, M_PASSES = D // 512, M // 512
PAIR = 2 * P

FLOPS = 2 * N * D * M + 2 * N * M * V + 2 * N * D * V

ORDER = """
round_identity; spread_kb 0-1; widen_s 0 4-7; widen_v 0 0-3; turn_h 0; keep_kb 0-1; copy_h_v 0 0; copy_h_s 0 1;
spread_kb 2-3; keep_kb 2-3; spread_g 0; quantize_h 0 0-1; widen_s 1 4-7; scores 0 0-1; widen_v 1 0-3; keep_g 0;
spread_g 1; add_kb 0 0-1; turn_h 1; copy_h_s 1 0-1; quantize_h 1 0-1; scores 0 2-3; add_kb 0 2-3; widen_s 2 0-7;
scores 1 0-3; keep_g 1; widen_s 3 0-7; add_kb 1 0; pair_max 0; turn_h 2; copy_h_s 2 0-1; turn_h 3; add_kb 1 1-3;
copy_h_s 3 0-1; quantize_h 2 0-1; row_max 0; pair_max 1; spread_g 2-3; quantize_h 3 0-1; row_max 1; keep_g 2-3;
scores 2 0-3; add_kb 2 0-2; exp_scores 0; exp_scores 1; invert_sum 0; add_kb 2 3; gain 0 0-1; scores 3 0-1;
logits 0 0-3; add_kb 3 0-1; copy_logits 0 0-3; scores 3 2; copied_logit_max 0; turn_a 0 0-1; copy_a 0 0-1;
quantize_a 0 0-1; scores 3 3; exp_logits 0 0-3; readout 0 0-3; pair_max 2; add_kb 3 2; row_max 2; invert_sum 1;
add_kb 3 3; drain 0 0; gain 1 0-1; turn_a 1 0-1; pair_max 3; exp_scores 2; invert_sum 2; drain 0 1-3; copy_a 1 0;
row_max 3; exp_scores 3; copy_a 1 1; logits 1 0-3; chunk_max 1 0-3; logits 2 0-3; quantize_a 1 0; gate_roots;
logit_max 1; invert_sum 3; chunk_max 2 0-2; exp_logits 1 0-3; gate_square; quantize_a 1 1; chunk_max 2 3;
gate_spread; gate_means; readout 1 0-2; gate_fourth; logit_max 2; gain 2 0; gate_odds; gain 2 1; turn_a 2 0-1;
exp_logits 2 0-3; logits 3 0-3; gate_odds_1; gain 3 0; gate_lam; sum_logits 0 2; copy_a 2 0-1; gate_less_1;
drain_gated 1 0-2; invert_logits 0 2; readout 1 3; quantize_a 2 0; chunk_max 3 0-1; gate_factor 0 2; chunk_max 3 2-3;
quantize_a 2 1; logit_max 3; readout 2 0-1; gain 3 1; turn_a 3 0-1; readout 2 2-3; mix 1 0 2; gate_prob 0;
mix_drained 0 0 2; mix_drained 0 2 4; exp_logits 3 0-3; sum_logits 2 4; copy_a 3 0-1; quantize_a 3 0;
drain_gated 1 3; invert_logits 2 4; quantize_a 3 1; readout 3 0-3; gate_factor 2 4; mix 1 2 4; drain_gated 2 0-3;
mix 2 0 2; drain_gated 3 0-3; mix 2 2 4; mix 3 0 2; mix 3 2 3; mix 3 3 4
"""


def tile_gatedmemoryattentionlmhead_kernel(
    tc, h_bytes, h_scale, keys_words, keys_scales, kb, g, val_words, val_scales, w_lm_words, w_lm_scales, out
):
    nc = tc.nc
    with ExitStack() as ctx:
        keep = ctx.enter_context(tc.tile_pool(name="keep", bufs=1))
        work = ctx.enter_context(tc.tile_pool(name="work", bufs=2))
        psum = ctx.enter_context(tc.psum_pool(name="psum", bufs=8))
        ctx.enter_context(tc.manual_schedule())

        h_codes_in = keep.tile([P, TILES, D], U8, name="h_codes_in", align_bytes=64)
        h_factors = keep.tile([P, TILES * BLOCKS], F32, name="h_factors")
        kb_rows = keep.tile([P, CHUNK], BF16, name="kb_rows")
        g_rows = keep.tile([P, CHUNK], BF16, name="g_rows")
        ident = keep.tile([P, P], F32, name="ident")
        ident_bf = keep.tile([P, P], BF16, name="ident_bf")
        ones = keep.tile([P, P], F32, name="ones")
        root = keep.tile([P, 1], F32, name="root")
        keys_planes = keep.tile([P, M], U8, name="keys_planes", align_bytes=64)
        w_lm_planes = keep.tile([P, V], U8, name="w_lm_planes", align_bytes=64)
        val_planes = keep.tile([P, V], U8, name="val_planes", align_bytes=64)
        keys_w = [keep.tile([P, D_PASSES, CHUNK], U32, name=f"keys_w{c}", align_bytes=64) for c in range(CHUNKS)]
        w_lm_w = [keep.tile([P, D_PASSES, CHUNK], U32, name=f"w_lm_w{c}", align_bytes=64) for c in range(CHUNKS)]
        val_w = [keep.tile([P, M_PASSES, CHUNK], U32, name=f"val_w{c}", align_bytes=64) for c in range(CHUNKS)]
        kb_all = keep.tile([P, M], BF16, name="kb_all")
        g8_all = keep.tile([P, 2, M // 4, 2], BF16, name="g8_all")
        h_q = [keep.tile([P, D_PASSES, P], U32, name=f"h_q{i}", align_bytes=64) for i in range(TILES)]
        h_s = [keep.tile([P, D_PASSES, P], U8, name=f"h_s{i}", align_bytes=64) for i in range(TILES)]
        neg_max = keep.tile([P, TILES], F32, name="neg_max")
        sums = keep.tile([P, TILES], F32, name="sums")
        inv_sums = keep.tile([P, TILES], F32, name="inv_sums")
        z_neg_max_chunk = keep.tile([P, TILES * CHUNKS], F32, name="z_neg_max_chunk")
        z_neg_max = keep.tile([P, TILES], F32, name="z_neg_max")
        z_sums_chunk = keep.tile([P, TILES * CHUNKS], F32, name="z_sums_chunk")
        z_sums = keep.tile([P, TILES], F32, name="z_sums")
        z_inv = keep.tile([P, TILES], F32, name="z_inv")
        lam = keep.tile([P, TILES], F32, name="lam")
        lam_less_1 = keep.tile([P, TILES], F32, name="lam_less_1")
        p_factor = keep.tile([P, TILES], F32, name="p_factor")
        sum_product = keep.tile([P, 1], F32, name="sum_product")
        sum_root = keep.tile([P, 1], F32, name="sum_root")
        mean_term = keep.tile([P, 1], F32, name="mean_term")
        root_product = keep.tile([P, 1], F32, name="root_product")
        inv_2 = keep.tile([P, TILES], F32, name="inv_2")
        inv_4 = keep.tile([P, TILES], F32, name="inv_4")
        odds_exp = keep.tile([P, TILES], F32, name="odds_exp")
        odds = keep.tile([P, TILES], F32, name="odds")
        few = keep.tile([P, TILES], F32, name="few")
        many = keep.tile([P, P], F32, name="many")

        h_bf, h_bank, h_pairs = {}, {}, {}
        spread, score_bank, logit_bank, turn_bank, readout_bank = {}, {}, {}, {}, {}
        scores_sb, half_max, w_exp, z_copy, prob, a_bf, a_pairs, a_q, a_s, mixed = {}, {}, {}, {}, {}, {}, {}, {}, {}, {}

        def made(tiles, i, shape, dtype, name, bufs):
            if i not in tiles:
                tiles[i] = work.tile(shape, dtype, name=name, align_bytes=64, bufs=bufs)
            return tiles[i]

        def new_bank():
            return psum.tile([P, CHUNK], F32, name="bank")

        def col(t, i):
            return t[:, i : i + 1]

        def chunk(c):
            return slice(c * CHUNK, (c + 1) * CHUNK)

        def load_words(tiles, words, c):
            view = words.rearrange("g p n t -> p g (n t)").bitcast(I32)
            nc.sync.dma_start(out=tiles[c][:].bitcast(I32), in_=view[:, :, chunk(c)])

        def load_scales(queue, planes, scales, passes):
            for q in range(4):
                queue.dma_start(
                    out=planes[32 * q : 32 * q + 4 * passes, :].bitcast(I32),
                    in_=scales.bitcast(I32)[:, 4 * q : 4 * q + 4, :],
                )

        h_rows = h_bytes.rearrange("(p i) k -> p i k", i=TILES)
        out_rows = out.rearrange("(p i) n -> p i n", i=TILES)
        as_rows = "(c n) -> c n"

        nc.vector.memset(keys_planes[:].bitcast(I32), 0)
        nc.vector.memset(kb_rows[:], 0.0)
        nc.vector.memset(ones[:], 0.0)
        nc.vector.memset(g_rows[:], 0.0)
        nc.vector.memset(w_lm_planes[:].bitcast(I32), 0)
        nc.vector.memset(val_planes[:].bitcast(I32), 0)
        nc.sync.dma_start(out=h_codes_in[:, 0, :], in_=h_rows[:, 0, :])
        nc.scalar.dma_start(out=h_factors[:], in_=h_scale.rearrange("(p i) b -> p (i b)", i=TILES))
        nc.scalar.dma_start(out=kb_rows[0:CHUNKS, :], in_=kb.rearrange(as_rows, c=CHUNKS))
        load_scales(nc.sync, keys_planes, keys_scales, D_PASSES)
        load_words(keys_w, keys_words, 0)
        load_words(keys_w, keys_words, 1)
        nc.sync.dma_start(out=h_codes_in[:, 1:TILES, :], in_=h_rows[:, 1:TILES, :])
        nc.scalar.dma_start(out=g_rows[0:CHUNKS, :], in_=g.rearrange(as_rows, c=CHUNKS))
        nc.scalar.activation(out=ones[:], in_=ones[:], func=ACT.Exp)
        make_identity(nc, ident[:])
        nc.gpsimd.memset(root[:], 1.0 / P)
        for c in range(2, CHUNKS):
            load_words(keys_w, keys_words, c)
        load_scales(nc.sync, w_lm_planes, w_lm_scales, D_PASSES)
        load_scales(nc.gpsimd, val_planes, val_scales, M_PASSES)
        for c in range(CHUNKS):
            load_words(w_lm_w, w_lm_words, c)
        for c in range(CHUNKS):
            load_words(val_w, val_words, c)

        def spread_row(rows, key, c):
            spread[key, c] = new_bank()
            nc.tensor.matmul(
                spread[key, c][:], lhsT=col(ident_bf, c).to_broadcast([P, P]), rhs=rows[:], start=True, stop=True
            )

        def round_identity():
            nc.vector.tensor_copy(out=ident_bf[:], in_=ident[:])

        def spread_kb(c):
            spread_row(kb_rows, "kb", c)

        def spread_g(c):
            spread_row(g_rows, "g", c)

        def keep_kb(c):
            nc.scalar.copy(out=kb_all[:, chunk(c)], in_=spread["kb", c][:])

        def keep_g(c):
            nc.scalar.activation(
                out=g8_all[:, :, c * P : (c + 1) * P, :],
                in_=spread["g", c][:].rearrange("p (w u e) -> p u w e", u=2, e=2),
                func=ACT.Copy,
                scale=8.0,
            )

        def widen(i, b):
            cols = slice(b * BLOCK, (b + 1) * BLOCK)
            h = made(h_bf, i, [P, D], BF16, "h_bf", 2)
            return h[:, cols], h_codes_in[:, i, cols].bitcast(FP8), col(h_factors, BLOCKS * i + b)

        def widen_v(i, b):
            to, codes, factor = widen(i, b)
            nc.vector.tensor_scalar(out=to, in0=codes, scalar1=factor, scalar2=None, op0=ALU.mult)

        def widen_s(i, b):
            to, codes, factor = widen(i, b)
            nc.scalar.activation(out=to, in_=codes, func=ACT.Copy, scale=factor)

        def turn_h(i):
            h_bank[i] = new_bank()
            turned = h_bank[i][:].rearrange("p (gu n) -> p gu n", n=P)
            words = h_bf[i][:].bitcast(F32)
            for gu in range(2 * D_PASSES):
                first = PAIR * (gu // 2)
                nc.tensor.transpose(turned[:, gu, :], words[:, first + gu % 2 : first + PAIR : 2], ident[:])

        def h_copy(i, q):
            pairs = made(h_pairs, i, [P, D_PASSES, 4 * P], BF16, "h_pairs", 2)
            to = pairs[:, q, :].bitcast(F32).rearrange("p (n u) -> p n u", u=2)
            return to, h_bank[i][:].rearrange("p (q u n) -> p q n u", u=2, n=P)[:, q, :, :]

        def copy_h_v(i, q):
            to, turned = h_copy(i, q)
            nc.vector.tensor_copy(out=to, in_=turned)

        def copy_h_s(i, q):
            to, turned = h_copy(i, q)
            nc.scalar.copy(out=to, in_=turned)

        def quantize_h(i, q):
            nc.vector.quantize_mx(out=h_q[i][:, q, :].bitcast(FP8X4), scales=h_s[i][:, q, :], in_=h_pairs[i][:, q, :])

        def product(bank, codes, scales, words, planes, passes, c):
            for q in range(passes):
                nc.tensor.matmul_mx(
                    out=bank[:],
                    lhsT=codes[:, q, :].bitcast(FP8X4),
                    lhsT_scale=scales[:, q, :],
                    rhs=words[c][:, q, :].bitcast(FP8X4),
                    rhs_scale=planes[4 * q : P, chunk(c)],
                    start=(q == 0),
                    stop=(q == passes - 1),
                )

        def scores(i, c):
            score_bank[i, c] = new_bank()
            product(score_bank[i, c], h_q[i], h_s[i], keys_w, keys_planes, D_PASSES, c)

        def logits(i, c):
            logit_bank[i, c] = new_bank()
            product(logit_bank[i, c], h_q[i], h_s[i], w_lm_w, w_lm_planes, D_PASSES, c)

        def readout(i, c):
            readout_bank[i, c] = new_bank()
            product(readout_bank[i, c], a_q[i], a_s[i], val_w, val_planes, M_PASSES, c)

        def add_kb(i, c):
            e = made(scores_sb, i, [P, CHUNKS, CHUNK], F32, "scores_sb", 3)
            nc.vector.scalar_tensor_tensor(
                out=e[:, c, :], in0=score_bank[i, c][:], scalar=1.0 / 20.0, in1=kb_all[:, chunk(c)], op0=ALU.mult, op1=ALU.add
            )

        def pair_max(i):
            t = made(half_max, i, [P, M // 2], BF16, "half_max", 2)
            nc.vector.tensor_tensor(
                out=t[:].rearrange("p (c n) -> p c n", c=2), in0=scores_sb[i][:, 0:2, :], in1=scores_sb[i][:, 2:4, :], op=ALU.max
            )

        def row_max(i):
            t = half_max[i][:]
            nc.vector.tensor_scalar(
                out=t, in0=t, scalar1=-1.0, scalar2=None, op0=ALU.mult, op1=ALU.min, accum_out=col(neg_max, i)
            )

        def exp_scores(i):
            w_exp[i] = work.tile([P, 2, M // 4, 2], F32, name="w_exp", bufs=3)
            nc.scalar.activation(
                out=w_exp[i][:],
                in_=scores_sb[i][:].rearrange("p c (w u e) -> p u (c w) e", u=2, e=2),
                func=ACT.Exp,
                bias=col(neg_max, i),
                accum_out=col(sums, i),
            )

        def invert_sum(i):
            nc.vector.reciprocal(out=col(inv_sums, i), in_=col(sums, i))

        def gain(i, half):
            a = made(a_bf, i, [P, 2, M // 2], BF16, "a_bf", 2)
            cols = slice(half * (M // 4), (half + 1) * (M // 4))
            nc.vector.scalar_tensor_tensor(
                out=a[:, :, cols],
                in0=w_exp[i][:].rearrange("p u w e -> p u (w e)")[:, :, cols],
                scalar=col(inv_sums, i),
                in1=g8_all[:].rearrange("p u w e -> p u (w e)")[:, :, cols],
                op0=ALU.mult,
                op1=ALU.mult,
            )

        def turn_a(i, half):
            turn_bank[i, half] = new_bank()
            turned = turn_bank[i, half][:].rearrange("p (q u n) -> p q u n", u=2, n=P)
            words = a_bf[i][:].bitcast(F32)
            for q in range(2):
                for u in range(2):
                    first = (2 * half + q) * P
                    nc.tensor.transpose(turned[:, q, u, :], words[:, u, first : first + P], ident[:])

        def copy_a(i, half):
            pairs = made(a_pairs, i, [P, M_PASSES, 4 * P], BF16, "a_pairs", 2)
            nc.scalar.copy(
                out=pairs[:, 2 * half : 2 * half + 2, :].bitcast(F32).rearrange("p q (n u) -> p q n u", u=2),
                in_=turn_bank[i, half][:].rearrange("p (q u n) -> p q n u", u=2, n=P),
            )

        def quantize_a(i, half):
            two = slice(2 * half, 2 * half + 2)
            codes = made(a_q, i, [P, M_PASSES, P], U32, "a_q", 4)
            scales = made(a_s, i, [P, M_PASSES, P], U8, "a_s", 4)
            nc.vector.quantize_mx(
                out=codes[:, two, :].rearrange("p q n -> p (q n)").bitcast(FP8X4),
                scales=scales[:, two, :].rearrange("p q n -> p (q n)"),
                in_=a_pairs[i][:, two, :].rearrange("p q k -> p (q k)"),
            )

        def chunk_max(i, c):
            nc.vector.tensor_reduce(
                out=col(z_neg_max_chunk, CHUNKS * i + c), in_=logit_bank[i, c][:], axis=AX.X, op=ALU.max, negate=True
            )

        def logit_max(i):
            chunks = z_neg_max_chunk[:, CHUNKS * i : CHUNKS * (i + 1)]
            nc.vector.tensor_reduce(out=col(z_neg_max, i), in_=chunks, axis=AX.X, op=ALU.min)

        def copy_logits(i, c):
            z = made(z_copy, i, [P, CHUNKS, CHUNK], BF16, "z_copy", 1)
            nc.scalar.copy(out=z[:, c, :], in_=logit_bank[i, c][:])

        def copied_logit_max(i):
            z = z_copy[i][:].rearrange("p c n -> p (c n)")
            nc.vector.tensor_scalar(
                out=z, in0=z, scalar1=-1.0, scalar2=None, op0=ALU.mult, op1=ALU.min, accum_out=col(z_neg_max, i)
            )

        def exp_logits(i, c):
            e = made(prob, i, [P, CHUNKS, CHUNK], F32, "prob", 4)
            nc.scalar.activation(
                out=e[:, c, :],
                in_=logit_bank[i, c][:],
                func=ACT.Exp,
                bias=col(z_neg_max, i),
                accum_out=col(z_sums_chunk, CHUNKS * i + c),
            )

        def sum_logits(lo, hi):
            chunks = z_sums_chunk[:, CHUNKS * lo : CHUNKS * hi].rearrange("p (i c) -> p i c", c=CHUNKS)
            nc.vector.tensor_reduce(out=z_sums[:, lo:hi], in_=chunks, axis=AX.X, op=ALU.add)

        def invert_logits(lo, hi):
            nc.vector.reciprocal(out=z_inv[:, lo:hi], in_=z_sums[:, lo:hi])

        def gate_roots():
            nc.vector.tensor_scalar(
                out=few[:], in0=sums[:], scalar1=1.0, scalar2=None, op0=ALU.mult, op1=ALU.mult, accum_out=sum_product[:]
            )
            nc.gpsimd.tensor_tensor(out=sum_root[:], in0=sum_product[:], in1=root[:], op=ALU.pow)

        def gate_square():
            nc.vector.tensor_tensor(out=inv_2[:], in0=inv_sums[:], in1=inv_sums[:], op=ALU.mult)

        def gate_fourth():
            nc.vector.tensor_tensor(out=inv_4[:], in0=inv_2[:], in1=inv_2[:], op=ALU.mult)

        def gate_spread():
            spread["gate"] = new_bank()
            nc.tensor.matmul(spread["gate"][:, P : P + TILES], lhsT=ones[:], rhs=neg_max[:], start=True, stop=True)
            nc.tensor.transpose(spread["gate"][:, 0:P], sum_root[:].to_broadcast([P, P]), ident[:])

        def gate_means():
            bank = spread["gate"]
            nc.vector.tensor_scalar(
                out=few[:],
                in0=bank[:, P : P + TILES],
                scalar1=-4.0 / N,
                scalar2=None,
                op0=ALU.mult,
                op1=ALU.add,
                accum_out=mean_term[:],
            )
            nc.vector.tensor_scalar(
                out=many[:], in0=bank[:, 0:P], scalar1=1.0, scalar2=None, op0=ALU.mult, op1=ALU.mult, accum_out=root_product[:]
            )
            nc.scalar.activation(out=odds_exp[:], in_=neg_max[:], func=ACT.Exp, scale=4.0, bias=mean_term[:])

        def gate_odds():
            nc.vector.tensor_tensor(out=odds[:], in0=odds_exp[:], in1=inv_4[:], op=ALU.mult)

        def gate_odds_1():
            nc.vector.tensor_scalar(
                out=odds[:], in0=odds[:], scalar1=root_product[:], scalar2=1.0, op0=ALU.mult, op1=ALU.add
            )

        def gate_lam():
            nc.vector.reciprocal(out=lam[:], in_=odds[:])

        def gate_less_1():
            nc.vector.tensor_scalar(out=lam_less_1[:], in0=lam[:], scalar1=-1.0, scalar2=None, op0=ALU.add)

        def gate_factor(lo, hi):
            nc.vector.scalar_tensor_tensor(
                out=p_factor[:, lo:hi], in0=lam_less_1[:, lo:hi], scalar=-float(V), in1=z_inv[:, lo:hi], op0=ALU.mult, op1=ALU.mult
            )

        def flat(t, lo, hi):
            return t[:, lo:hi, :].rearrange("p c n -> p (c n)")

        def store(i, lo, hi):
            nc.sync.dma_start(out=out_rows[:, i, lo * CHUNK : hi * CHUNK], in_=flat(mixed[i], lo, hi))

        def drain(i, c):
            o = made(mixed, i, [P, CHUNKS, CHUNK], F32, "mixed", 2)
            nc.scalar.copy(out=o[:, c, :], in_=readout_bank[i, c][:])

        def gate_prob(i):
            p = flat(prob[i], 0, CHUNKS)
            nc.scalar.activation(out=p, in_=p, func=ACT.Identity, scale=col(p_factor, i), bias=col(lam_less_1, i))

        def mix_drained(i, lo, hi):
            o = flat(mixed[i], lo, hi)
            nc.vector.scalar_tensor_tensor(
                out=o, in0=o, scalar=col(lam, i), in1=flat(prob[i], lo, hi), op0=ALU.mult, op1=ALU.add
            )
            store(i, lo, hi)

        def drain_gated(i, c):
            o = made(mixed, i, [P, CHUNKS, CHUNK], F32, "mixed", 2)
            nc.scalar.activation(
                out=o[:, c, :], in_=readout_bank[i, c][:], func=ACT.Identity, scale=col(lam, i), bias=col(lam_less_1, i)
            )

        def mix(i, lo, hi):
            o = flat(mixed[i], lo, hi)
            nc.vector.scalar_tensor_tensor(
                out=o, in0=flat(prob[i], lo, hi), scalar=col(p_factor, i), in1=o, op0=ALU.mult, op1=ALU.add
            )
            store(i, lo, hi)

        steps = {
            "widen_v": widen_v, "widen_s": widen_s, "round_identity": round_identity, "spread_kb": spread_kb,
            "spread_g": spread_g, "keep_kb": keep_kb, "keep_g": keep_g, "turn_h": turn_h, "copy_h_v": copy_h_v,
            "copy_h_s": copy_h_s, "quantize_h": quantize_h, "scores": scores, "logits": logits, "readout": readout,
            "add_kb": add_kb, "pair_max": pair_max, "row_max": row_max, "exp_scores": exp_scores,
            "invert_sum": invert_sum, "gain": gain, "turn_a": turn_a, "copy_a": copy_a, "quantize_a": quantize_a,
            "chunk_max": chunk_max, "logit_max": logit_max, "copy_logits": copy_logits,
            "copied_logit_max": copied_logit_max, "exp_logits": exp_logits, "sum_logits": sum_logits,
            "invert_logits": invert_logits, "gate_roots": gate_roots, "gate_square": gate_square,
            "gate_fourth": gate_fourth, "gate_spread": gate_spread, "gate_means": gate_means, "gate_odds": gate_odds,
            "gate_odds_1": gate_odds_1, "gate_lam": gate_lam, "gate_less_1": gate_less_1, "gate_factor": gate_factor,
            "drain": drain, "gate_prob": gate_prob, "mix_drained": mix_drained, "drain_gated": drain_gated,
            "mix": mix,
        }
        for entry in ORDER.replace("\n", " ").split(";"):
            words = entry.split()
            step, fixed, last = steps[words[0]], [int(w) for w in words[1:-1]], words[-1].split("-")
            if len(words) == 1:
                step()
            elif len(last) == 1:
                step(*fixed, int(last[0]))
            else:
                for index in range(int(last[0]), int(last[1]) + 1):
                    step(*fixed, index)
